import numpy as np
import ml_dtypes


def mxq(x, axis, fmt="e4m3"):
    dtype, down = {"e4m3": (ml_dtypes.float8_e4m3fn, 7), "e5m2": (ml_dtypes.float8_e5m2, 14)}[fmt]
    v = np.moveaxis(np.asarray(x, np.float32).astype(ml_dtypes.bfloat16).astype(np.float64), axis, -1)
    blocks = v.reshape(v.shape[:-1] + (-1, 32))
    amax = np.abs(blocks).max(-1, keepdims=True)
    byte = np.maximum(np.where(amax > 0, np.frexp(amax)[1] - 1 + 127, 0) - down, 1)
    scale = np.exp2(byte - 127.0)
    codes = (blocks / scale).astype(np.float32).astype(dtype).astype(np.float64)
    return np.moveaxis((codes * scale).reshape(v.shape), -1, axis)


WIDE = False


def mx_kscale(k):
    if not WIDE:
        return np.ones(k)
    levels = np.array([10, -10, 5, -5, 0])
    if k % 512:
        return np.exp2(np.random.permutation(np.resize(levels, k // 32))).repeat(32)
    a = np.empty((k // 512, 16))
    for p in range(k // 512):
        a[p, :8] = np.random.permutation(np.resize(levels, 8))
        for g in range(8):
            far = levels[np.abs(levels - a[p, g]) >= 10]
            a[p, g + 8] = far[np.random.randint(len(far))]
    return np.exp2(a.ravel()).repeat(32)


def f64(x):
    return np.asarray(x).astype(np.float64)


def striped(idx):
    return np.tile(idx.reshape(-1, 16).T, (8, 1)).astype(np.uint16)


def unstriped(offs):
    return offs[:16].T.reshape(-1).astype(np.int64)


def sigmoid(v):
    return 1.0 / (1.0 + np.exp(-np.maximum(v, -700.0)))


K, T, S, V, N = 512, 4096, 1024, 512, 256


def setup_inputs():
    n = np.random.standard_normal
    s = mx_kscale(K)[:, None]
    return {
        "xT": (n((K, T)) * s).astype(np.float32),
        "w1": (n((K, N)) / np.sqrt(K) / s).astype(np.float32),
        "w2": (n((K, N)) / np.sqrt(K) / s).astype(np.float32),
        "w3": (n((K, N)) / np.sqrt(K) / s).astype(np.float32),
        "offs": striped(np.random.permutation(T)[:S]),
        "cen": striped(np.random.permutation(S)[:V]),
        "pos1": striped(np.random.permutation(S)[:V]),
        "pos2": striped(np.random.permutation(S)[:V]),
    }


def reference(xT, w1, w2, w3, offs, cen, pos1, pos2):
    xq = mxq(f64(xT)[:, unstriped(offs)], 0, "e4m3")
    y = mxq(f64(w1), 0, "e4m3").T @ xq
    yc = y[:, unstriped(cen)]
    e = mxq(f64(w2), 0, "e4m3").T @ xq
    h = mxq(f64(w3), 0, "e4m3").T @ xq
    z = (sigmoid(yc + e[:, unstriped(pos1)])) * h[:, unstriped(pos1)] + (sigmoid(yc + e[:, unstriped(pos2)])) * h[:, unstriped(pos2)]
    return z

@@ -1,0 +1,129 @@
+from contextlib import ExitStack
+
+import concourse.mybir as mybir
+
+K, T, S, V, N = 512, 4096, 1024, 512, 256
+FLOPS = 3 * 2 * K * N * S
+
+F32 = mybir.dt.float32
+BF16 = mybir.dt.bfloat16
+U32 = mybir.dt.uint32
+U16 = mybir.dt.uint16
+U8 = mybir.dt.uint8
+FP8X4 = mybir.dt.float8_e4m3fn_x4
+ADD = mybir.AluOpType.add
+MULT = mybir.AluOpType.mult
+SIGMOID = mybir.ActivationFunctionType.Sigmoid
+
+P = 128
+PACK = 4
+HALF = 512
+HALVES = S // HALF
+BLOCKS = N // P
+STRIPE = 16
+
+
+def tile_picked_gatedg_none_e_kernel(tc, xT, w1, w2, w3, offs, cen, pos1, pos2, out):
+    nc = tc.nc
+    with ExitStack() as ctx:
+        lists = ctx.enter_context(tc.tile_pool(name="lists", bufs=1))
+        keep = ctx.enter_context(tc.tile_pool(name="keep", bufs=1))
+        psum = ctx.enter_context(tc.psum_pool(name="psum", bufs=8))
+
+        warm_in = keep.tile([P, 1], F32, name="warm_in")
+        warm_out = keep.tile([P, 1], F32, name="warm_out")
+        nc.vector.memset(warm_in[:], 0.0)
+        nc.scalar.activation(warm_out[:], warm_in[:], SIGMOID)
+
+        offs_t = lists.tile([P, S // STRIPE], U16, name="offs_t")
+        cen_t = lists.tile([P, V // STRIPE], U16, name="cen_t")
+        pos_t = [lists.tile([P, V // STRIPE], U16, name=f"pos_t{d}") for d in range(2)]
+        planes = [keep.tile([P, T], F32, name=f"plane{j}") for j in range(PACK)]
+        w_raw = [keep.tile([P, PACK, N], F32, name=f"w_raw{i}") for i in range(3)]
+        x_rows = xT.rearrange("(p j) t -> p j t", j=PACK)
+
+        def load_w(i, w):
+            nc.sync.dma_start(out=w_raw[i][:], in_=w.rearrange("(p j) n -> p j n", j=PACK))
+
+        nc.sync.dma_start(out=planes[0][:], in_=x_rows[:, 0, :])
+        nc.sync.dma_start(offs_t[:], offs)
+        for j in range(1, PACK):
+            nc.sync.dma_start(out=planes[j][:], in_=x_rows[:, j, :])
+        load_w(0, w1)
+        load_w(1, w2)
+        nc.sync.dma_start(cen_t[:], cen)
+        nc.sync.dma_start(pos_t[0][:], pos1)
+        load_w(2, w3)
+        nc.sync.dma_start(pos_t[1][:], pos2)
+
+        grouped = [keep.tile([P, HALF, PACK], BF16, name=f"grouped{u}", align_bytes=64) for u in range(HALVES)]
+        x_codes = [keep.tile([P, HALF], U32, name=f"x_codes{u}", align_bytes=64) for u in range(HALVES)]
+        x_scales = [keep.tile([P, HALF], U8, name=f"x_scales{u}", align_bytes=64) for u in range(HALVES)]
+        w_grouped = [keep.tile([P, N, PACK], BF16, name=f"w_grouped{i}", align_bytes=64) for i in range(3)]
+        w_codes = [keep.tile([P, N], U32, name=f"w_codes{i}", align_bytes=64) for i in range(3)]
+        w_scales = [keep.tile([P, N], U8, name=f"w_scales{i}", align_bytes=64) for i in range(3)]
+        res = [[keep.tile([P, S], F32, name=f"res{i}_{b}") for b in range(BLOCKS)] for i in range(3)]
+
+        def gather_x(j, u):
+            cols = slice(u * HALF // STRIPE, (u + 1) * HALF // STRIPE)
+            nc.vector.tensor_copy(grouped[u][:, :, j], planes[j][:].indirect(offs_t[:, cols]))
+
+        def quantize(codes, scales, values):
+            nc.vector.quantize_mx(out=codes[:].bitcast(FP8X4), scales=scales[:], in_=values[:].rearrange("p c j -> p (c j)"))
+
+        def interleave_w(i):
+            nc.scalar.copy(w_grouped[i][:].rearrange("p (c n) j -> p c j n", n=4), w_raw[i][:].rearrange("p j (c n) -> p c j n", n=4))
+
+        def product(i, b, u, on_vector):
+            acc = psum.tile([P, HALF], F32, name="acc")
+            rows = slice(b * P, (b + 1) * P)
+            nc.tensor.matmul_mx(out=acc[:], lhsT=w_codes[i][:, rows].bitcast(FP8X4), lhsT_scale=w_scales[i][:, rows],
+                                rhs=x_codes[u][:].bitcast(FP8X4), rhs_scale=x_scales[u][:], start=True, stop=True)
+            dst = res[i][b][:, u * HALF:(u + 1) * HALF]
+            if on_vector:
+                nc.vector.tensor_copy(dst, acc[:])
+            else:
+                nc.scalar.copy(dst, acc[:])
+
+        for j in range(PACK - 1):
+            for u in range(HALVES):
+                gather_x(j, u)
+        gather_x(PACK - 1, 0)
+        interleave_w(0)
+        interleave_w(1)
+        gather_x(PACK - 1, 1)
+        quantize(x_codes[0], x_scales[0], grouped[0])
+        quantize(w_codes[0], w_scales[0], w_grouped[0])
+        quantize(x_codes[1], x_scales[1], grouped[1])
+        quantize(w_codes[1], w_scales[1], w_grouped[1])
+        product(0, 0, 0, False)
+        product(0, 0, 1, True)
+        product(1, 0, 0, False)
+        product(1, 0, 1, False)
+        interleave_w(2)
+        quantize(w_codes[2], w_scales[2], w_grouped[2])
+
+        for b in range(BLOCKS):
+            if b > 0:
+                for i in range(2):
+                    for u in range(HALVES):
+                        product(i, b, u, False)
+            for u in range(HALVES):
+                product(2, b, u, False)
+            yc = keep.tile([P, V], F32, name=f"yc{b}")
+            nc.vector.tensor_copy(yc[:], res[0][b][:].indirect(cen_t[:]))
+            gate = []
+            for d in range(2):
+                pre = keep.tile([P, V], F32, name=f"pre{b}_{d}")
+                nc.vector.tensor_tensor(pre[:], res[1][b][:].indirect(pos_t[d][:]), yc[:], ADD)
+                g = keep.tile([P, V], F32, name=f"gate{b}_{d}")
+                nc.scalar.activation(g[:], pre[:], SIGMOID)
+                gate.append(g)
+            msg = []
+            for d in range(2):
+                m = keep.tile([P, V], F32, name=f"msg{b}_{d}")
+                nc.vector.tensor_tensor(m[:], res[2][b][:].indirect(pos_t[d][:]), gate[d][:], MULT)
+                msg.append(m)
+            z = keep.tile([P, V], F32, name=f"z{b}")
+            nc.vector.tensor_tensor(z[:], msg[0][:], msg[1][:], ADD)
+            nc.sync.dma_start(out=out[b * P:(b + 1) * P, :], in_=z[:])

@@ -1,6 +1,7 @@
 from contextlib import ExitStack
 
 import concourse.mybir as mybir
+from concourse.masks import make_identity
 
 K, T, S, V, N = 512, 4096, 1024, 512, 256
 FLOPS = 3 * 2 * K * N * S
@@ -14,6 +15,7 @@ FP8X4 = mybir.dt.float8_e4m3fn_x4
 ADD = mybir.AluOpType.add
 MULT = mybir.AluOpType.mult
 SIGMOID = mybir.ActivationFunctionType.Sigmoid
+COPY = mybir.ActivationFunctionType.Copy
 
 P = 128
 PACK = 4
@@ -21,6 +23,7 @@ HALF = 512
 HALVES = S // HALF
 BLOCKS = N // P
 STRIPE = 16
+CHUNKS = ((0, 1024), (1024, 2048), (2048, 3072), (3072, 3712), (3712, 4096))
 
 
 def tile_picked_gatedg_none_e_kernel(tc, xT, w1, w2, w3, offs, cen, pos1, pos2, out):
@@ -35,6 +38,9 @@ def tile_picked_gatedg_none_e_kernel(tc, xT, w1, w2, w3, offs, cen, pos1, pos2, 
         nc.vector.memset(warm_in[:], 0.0)
         nc.scalar.activation(warm_out[:], warm_in[:], SIGMOID)
 
+        identity = keep.tile([P, P], F32, name="identity")
+        make_identity(nc, identity[:])
+
         offs_t = lists.tile([P, S // STRIPE], U16, name="offs_t")
         cen_t = lists.tile([P, V // STRIPE], U16, name="cen_t")
         pos_t = [lists.tile([P, V // STRIPE], U16, name=f"pos_t{d}") for d in range(2)]
@@ -47,18 +53,21 @@ def tile_picked_gatedg_none_e_kernel(tc, xT, w1, w2, w3, offs, cen, pos1, pos2, 
 
         nc.sync.dma_start(out=planes[0][:], in_=x_rows[:, 0, :])
         nc.sync.dma_start(offs_t[:], offs)
-        for j in range(1, PACK):
+        for j in range(1, PACK - 1):
             nc.sync.dma_start(out=planes[j][:], in_=x_rows[:, j, :])
         load_w(0, w1)
+        for first, last in CHUNKS:
+            nc.sync.dma_start(out=planes[PACK - 1][:, first:last], in_=x_rows[:, PACK - 1, first:last])
         load_w(1, w2)
         nc.sync.dma_start(cen_t[:], cen)
         nc.sync.dma_start(pos_t[0][:], pos1)
         load_w(2, w3)
         nc.sync.dma_start(pos_t[1][:], pos2)
+        rounded = keep.tile([P, T], BF16, name="rounded")
 
         grouped = [keep.tile([P, HALF, PACK], BF16, name=f"grouped{u}", align_bytes=64) for u in range(HALVES)]
-        x_codes = [keep.tile([P, HALF], U32, name=f"x_codes{u}", align_bytes=64) for u in range(HALVES)]
-        x_scales = [keep.tile([P, HALF], U8, name=f"x_scales{u}", align_bytes=64) for u in range(HALVES)]
+        x_codes = keep.tile([P, S], U32, name="x_codes", align_bytes=64)
+        x_scales = keep.tile([P, S], U8, name="x_scales", align_bytes=64)
         w_grouped = [keep.tile([P, N, PACK], BF16, name=f"w_grouped{i}", align_bytes=64) for i in range(3)]
         w_codes = [keep.tile([P, N], U32, name=f"w_codes{i}", align_bytes=64) for i in range(3)]
         w_scales = [keep.tile([P, N], U8, name=f"w_scales{i}", align_bytes=64) for i in range(3)]
@@ -69,61 +78,112 @@ def tile_picked_gatedg_none_e_kernel(tc, xT, w1, w2, w3, offs, cen, pos1, pos2, 
             nc.vector.tensor_copy(grouped[u][:, :, j], planes[j][:].indirect(offs_t[:, cols]))
 
         def quantize(codes, scales, values):
-            nc.vector.quantize_mx(out=codes[:].bitcast(FP8X4), scales=scales[:], in_=values[:].rearrange("p c j -> p (c j)"))
+            nc.vector.quantize_mx(out=codes.bitcast(FP8X4), scales=scales, in_=values.rearrange("p c j -> p (c j)"))
 
-        def interleave_w(i):
-            nc.scalar.copy(w_grouped[i][:].rearrange("p (c n) j -> p c j n", n=4), w_raw[i][:].rearrange("p j (c n) -> p c j n", n=4))
+        def quantize_x(first, last):
+            u = first // HALF
+            quantize(x_codes[:, first:last], x_scales[:, first:last], grouped[u][:, first - u * HALF:last - u * HALF, :])
 
-        def product(i, b, u, on_vector):
+        def quantize_w(i, first=0, last=N):
+            quantize(w_codes[i][:, first:last], w_scales[i][:, first:last], w_grouped[i][:, first:last, :])
+
+        def interleave_w(i, first=0, last=N):
+            nc.scalar.copy(w_grouped[i][:, first:last, :].rearrange("p (c n) j -> p c j n", n=4),
+                           w_raw[i][:, :, first:last].rearrange("p j (c n) -> p c j n", n=4))
+
+        def product(i, b, first, last, on_vector=False):
             acc = psum.tile([P, HALF], F32, name="acc")
             rows = slice(b * P, (b + 1) * P)
-            nc.tensor.matmul_mx(out=acc[:], lhsT=w_codes[i][:, rows].bitcast(FP8X4), lhsT_scale=w_scales[i][:, rows],
-                                rhs=x_codes[u][:].bitcast(FP8X4), rhs_scale=x_scales[u][:], start=True, stop=True)
-            dst = res[i][b][:, u * HALF:(u + 1) * HALF]
+            nc.tensor.matmul_mx(out=acc[:, :last - first], lhsT=w_codes[i][:, rows].bitcast(FP8X4), lhsT_scale=w_scales[i][:, rows],
+                                rhs=x_codes[:, first:last].bitcast(FP8X4), rhs_scale=x_scales[:, first:last], start=True, stop=True)
+            dst = res[i][b][:, first:last]
             if on_vector:
-                nc.vector.tensor_copy(dst, acc[:])
+                nc.vector.tensor_copy(dst, acc[:, :last - first])
             else:
-                nc.scalar.copy(dst, acc[:])
+                nc.scalar.copy(dst, acc[:, :last - first])
+
+        def tiles(stem):
+            return [[keep.tile([P, V], F32, name=f"{stem}{b}_{d}") for d in range(2)] for b in range(BLOCKS)]
+
+        yc = [keep.tile([P, V], F32, name=f"yc{b}") for b in range(BLOCKS)]
+        z = [keep.tile([P, V], F32, name=f"z{b}") for b in range(BLOCKS)]
+        pre, gate, msg = tiles("pre"), tiles("gate"), tiles("msg")
+
+        def message(b, d, first=0, last=V):
+            nc.vector.tensor_tensor(msg[b][d][:, first:last], res[2][b][:].indirect(pos_t[d][:, first // STRIPE:last // STRIPE]),
+                                    gate[b][d][:, first:last], MULT)
+
+        def finish(b, queue, first=0, last=V):
+            nc.vector.tensor_tensor(z[b][:, first:last], msg[b][0][:, first:last], msg[b][1][:, first:last], ADD)
+            queue.dma_start(out=out[b * P:(b + 1) * P, first:last], in_=z[b][:, first:last])
+
+        turned_sb = keep.tile([P, V], F32, name="turned_sb")
+
+        def finish_on_tensor(b, first, last):
+            squares = [slice(c, c + P) for c in range(first, last, P)]
+            turned = psum.tile([P, HALF], F32, name="acc")
+            for d in range(2):
+                for c, cols in enumerate(squares):
+                    nc.tensor.matmul(turned[:, cols], msg[b][d][:, cols], identity[:], is_transpose=True,
+                                     start=(d == 0 and c == 0), stop=(d == 1 and c == len(squares) - 1))
+            nc.scalar.copy(turned_sb[:, first:last], turned[:, first:last])
+            back = psum.tile([P, HALF], F32, name="acc")
+            for cols in squares:
+                nc.tensor.transpose(back[:, cols], turned_sb[:, cols], identity[:])
+            nc.scalar.copy(z[b][:, first:last], back[:, first:last])
+            nc.sync.dma_start(out=out[b * P:(b + 1) * P, first:last], in_=z[b][:, first:last])
+
+        def centre(b):
+            nc.vector.tensor_copy(yc[b][:], res[0][b][:].indirect(cen_t[:]))
+
+        def gating(b, d):
+            nc.vector.tensor_tensor(pre[b][d][:], res[1][b][:].indirect(pos_t[d][:]), yc[b][:], ADD)
+            nc.scalar.activation(gate[b][d][:], pre[b][d][:], SIGMOID)
+
+        def both(i, b):
+            for u in range(HALVES):
+                product(i, b, u * HALF, (u + 1) * HALF)
 
         for j in range(PACK - 1):
             for u in range(HALVES):
                 gather_x(j, u)
-        gather_x(PACK - 1, 0)
         interleave_w(0)
+        quantize_w(0)
+        for c, (first, last) in enumerate(CHUNKS):
+            if c in (2, 3,):
+                nc.vector.tensor_copy(rounded[:, first:last], planes[PACK - 1][:, first:last])
+            else:
+                nc.scalar.copy(rounded[:, first:last], planes[PACK - 1][:, first:last])
+        gather_x(PACK - 1, 0)
+        nc.scalar.activation(grouped[1][:, :, PACK - 1], rounded[:].indirect(offs_t[:, HALF // STRIPE:]), COPY)
+        quantize_x(0, 512)
         interleave_w(1)
-        gather_x(PACK - 1, 1)
-        quantize(x_codes[0], x_scales[0], grouped[0])
-        quantize(w_codes[0], w_scales[0], w_grouped[0])
-        quantize(x_codes[1], x_scales[1], grouped[1])
-        quantize(w_codes[1], w_scales[1], w_grouped[1])
-        product(0, 0, 0, False)
-        product(0, 0, 1, True)
-        product(1, 0, 0, False)
-        product(1, 0, 1, False)
         interleave_w(2)
-        quantize(w_codes[2], w_scales[2], w_grouped[2])
-
-        for b in range(BLOCKS):
-            if b > 0:
-                for i in range(2):
-                    for u in range(HALVES):
-                        product(i, b, u, False)
-            for u in range(HALVES):
-                product(2, b, u, False)
-            yc = keep.tile([P, V], F32, name=f"yc{b}")
-            nc.vector.tensor_copy(yc[:], res[0][b][:].indirect(cen_t[:]))
-            gate = []
-            for d in range(2):
-                pre = keep.tile([P, V], F32, name=f"pre{b}_{d}")
-                nc.vector.tensor_tensor(pre[:], res[1][b][:].indirect(pos_t[d][:]), yc[:], ADD)
-                g = keep.tile([P, V], F32, name=f"gate{b}_{d}")
-                nc.scalar.activation(g[:], pre[:], SIGMOID)
-                gate.append(g)
-            msg = []
-            for d in range(2):
-                m = keep.tile([P, V], F32, name=f"msg{b}_{d}")
-                nc.vector.tensor_tensor(m[:], res[2][b][:].indirect(pos_t[d][:]), gate[d][:], MULT)
-                msg.append(m)
-            z = keep.tile([P, V], F32, name=f"z{b}")
-            nc.vector.tensor_tensor(z[:], msg[0][:], msg[1][:], ADD)
-            nc.sync.dma_start(out=out[b * P:(b + 1) * P, :], in_=z[:])
+        quantize_x(512, 768)
+        quantize_x(768, 1024)
+        product(0, 0, 0, 512, True)
+        quantize_w(1)
+        product(0, 0, 512, 768, True)
+        product(0, 0, 768, 1024, True)
+        quantize_w(2)
+        both(0, 1)
+        both(1, 0)
+        both(1, 1)
+        both(2, 0)
+        both(2, 1)
+        centre(0)
+        centre(1)
+        gating(0, 0)
+        gating(0, 1)
+        gating(1, 0)
+        gating(1, 1)
+        message(0, 0)
+        message(0, 1, 0, 256)
+        message(0, 1, 256, 512)
+        finish_on_tensor(0, 0, 256)
+        finish_on_tensor(0, 256, 512)
+        message(1, 0)
+        message(1, 1, 0, 256)
+        message(1, 1, 256, 512)
+        finish(1, nc.sync, 0, 256)
+        finish(1, nc.scalar, 256, 512)

@@ -119,7 +119,7 @@ def tile_picked_gatedg_none_e_kernel(tc, xT, w1, w2, w3, offs, cen, pos1, pos2, 
 
         turned_sb = keep.tile([P, V], F32, name="turned_sb")
 
-        def finish_on_tensor(b, first, last):
+        def add_turned(b, first, last):
             squares = [slice(c, c + P) for c in range(first, last, P)]
             turned = psum.tile([P, HALF], F32, name="acc")
             for d in range(2):
@@ -127,11 +127,13 @@ def tile_picked_gatedg_none_e_kernel(tc, xT, w1, w2, w3, offs, cen, pos1, pos2, 
                     nc.tensor.matmul(turned[:, cols], msg[b][d][:, cols], identity[:], is_transpose=True,
                                      start=(d == 0 and c == 0), stop=(d == 1 and c == len(squares) - 1))
             nc.scalar.copy(turned_sb[:, first:last], turned[:, first:last])
+
+        def turn_back(b, first, last):
             back = psum.tile([P, HALF], F32, name="acc")
-            for cols in squares:
-                nc.tensor.transpose(back[:, cols], turned_sb[:, cols], identity[:])
+            for c in range(first, last, P):
+                nc.tensor.transpose(back[:, c:c + P], turned_sb[:, c:c + P], identity[:])
             nc.scalar.copy(z[b][:, first:last], back[:, first:last])
-            nc.sync.dma_start(out=out[b * P:(b + 1) * P, first:last], in_=z[b][:, first:last])
+            nc.scalar.dma_start(out=out[b * P:(b + 1) * P, first:last], in_=z[b][:, first:last])
 
         def centre(b):
             nc.vector.tensor_copy(yc[b][:], res[0][b][:].indirect(cen_t[:]))
@@ -170,20 +172,24 @@ def tile_picked_gatedg_none_e_kernel(tc, xT, w1, w2, w3, offs, cen, pos1, pos2, 
         both(1, 0)
         both(1, 1)
         both(2, 0)
-        both(2, 1)
         centre(0)
         centre(1)
+        shared = keep.tile([P, V + V // 2], F32, name="shared")
+        gate[0][1] = shared[:, V // 2:]
+        pre[1][1] = shared[:, :V]
         gating(0, 0)
         gating(0, 1)
+        both(2, 1)
         gating(1, 0)
-        gating(1, 1)
         message(0, 0)
         message(0, 1, 0, 256)
         message(0, 1, 256, 512)
-        finish_on_tensor(0, 0, 256)
-        finish_on_tensor(0, 256, 512)
+        add_turned(0, 0, 256)
+        add_turned(0, 256, 512)
+        gating(1, 1)
+        turn_back(0, 0, 512)
         message(1, 0)
         message(1, 1, 0, 256)
         message(1, 1, 256, 512)
         finish(1, nc.sync, 0, 256)
-        finish(1, nc.scalar, 256, 512)
+        finish(1, nc.sync, 256, 512)

@@ -19,11 +19,19 @@ COPY = mybir.ActivationFunctionType.Copy
 
 P = 128
 PACK = 4
-HALF = 512
-HALVES = S // HALF
-BLOCKS = N // P
+LAST = PACK - 1
 STRIPE = 16
-CHUNKS = ((0, 1024), (1024, 2048), (2048, 3072), (3072, 3712), (3712, 4096))
+BANK = 512
+BANKS = 8
+HALF = S // 2
+QUARTER = S // 4
+MID = V // 2
+BLOCKS = N // P
+NEIGHBOURS = 2
+Y, E, H = 0, 1, 2
+RUN = 4
+
+CHUNKS = ((0, 1024, False), (1024, 2048, False), (2048, 3072, True), (3072, 3712, True), (3712, T, False))
 
 
 def tile_picked_gatedg_none_e_kernel(tc, xT, w1, w2, w3, offs, cen, pos1, pos2, out):
@@ -31,21 +39,16 @@ def tile_picked_gatedg_none_e_kernel(tc, xT, w1, w2, w3, offs, cen, pos1, pos2, 
     with ExitStack() as ctx:
         lists = ctx.enter_context(tc.tile_pool(name="lists", bufs=1))
         keep = ctx.enter_context(tc.tile_pool(name="keep", bufs=1))
-        psum = ctx.enter_context(tc.psum_pool(name="psum", bufs=8))
-
-        warm_in = keep.tile([P, 1], F32, name="warm_in")
-        warm_out = keep.tile([P, 1], F32, name="warm_out")
-        nc.vector.memset(warm_in[:], 0.0)
-        nc.scalar.activation(warm_out[:], warm_in[:], SIGMOID)
+        psum = ctx.enter_context(tc.psum_pool(name="psum", bufs=BANKS))
 
         identity = keep.tile([P, P], F32, name="identity")
         make_identity(nc, identity[:])
 
         offs_t = lists.tile([P, S // STRIPE], U16, name="offs_t")
         cen_t = lists.tile([P, V // STRIPE], U16, name="cen_t")
-        pos_t = [lists.tile([P, V // STRIPE], U16, name=f"pos_t{d}") for d in range(2)]
+        pos_t = [lists.tile([P, V // STRIPE], U16, name=f"pos_t{d}") for d in range(NEIGHBOURS)]
         planes = [keep.tile([P, T], F32, name=f"plane{j}") for j in range(PACK)]
-        w_raw = [keep.tile([P, PACK, N], F32, name=f"w_raw{i}") for i in range(3)]
+        w_raw = [keep.tile([P, PACK, N], F32, name=f"w_raw{i}") for i in (Y, E, H)]
         x_rows = xT.rearrange("(p j) t -> p j t", j=PACK)
 
         def load_w(i, w):
@@ -53,29 +56,40 @@ def tile_picked_gatedg_none_e_kernel(tc, xT, w1, w2, w3, offs, cen, pos1, pos2, 
 
         nc.sync.dma_start(out=planes[0][:], in_=x_rows[:, 0, :])
         nc.sync.dma_start(offs_t[:], offs)
-        for j in range(1, PACK - 1):
+        for j in range(1, LAST):
             nc.sync.dma_start(out=planes[j][:], in_=x_rows[:, j, :])
-        load_w(0, w1)
-        for first, last in CHUNKS:
-            nc.sync.dma_start(out=planes[PACK - 1][:, first:last], in_=x_rows[:, PACK - 1, first:last])
-        load_w(1, w2)
+        load_w(Y, w1)
+        for first, last, on_vector in CHUNKS:
+            nc.sync.dma_start(out=planes[LAST][:, first:last], in_=x_rows[:, LAST, first:last])
+        load_w(E, w2)
         nc.sync.dma_start(cen_t[:], cen)
         nc.sync.dma_start(pos_t[0][:], pos1)
-        load_w(2, w3)
+        load_w(H, w3)
         nc.sync.dma_start(pos_t[1][:], pos2)
-        rounded = keep.tile([P, T], BF16, name="rounded")
 
-        grouped = [keep.tile([P, HALF, PACK], BF16, name=f"grouped{u}", align_bytes=64) for u in range(HALVES)]
+        rounded = keep.tile([P, T], BF16, name="rounded")
+        grouped = [keep.tile([P, HALF, PACK], BF16, name=f"grouped{u}", align_bytes=64) for u in range(S // HALF)]
         x_codes = keep.tile([P, S], U32, name="x_codes", align_bytes=64)
         x_scales = keep.tile([P, S], U8, name="x_scales", align_bytes=64)
-        w_grouped = [keep.tile([P, N, PACK], BF16, name=f"w_grouped{i}", align_bytes=64) for i in range(3)]
-        w_codes = [keep.tile([P, N], U32, name=f"w_codes{i}", align_bytes=64) for i in range(3)]
-        w_scales = [keep.tile([P, N], U8, name=f"w_scales{i}", align_bytes=64) for i in range(3)]
-        res = [[keep.tile([P, S], F32, name=f"res{i}_{b}") for b in range(BLOCKS)] for i in range(3)]
+        w_grouped = [keep.tile([P, N, PACK], BF16, name=f"w_grouped{i}", align_bytes=64) for i in (Y, E, H)]
+        w_codes = [keep.tile([P, N], U32, name=f"w_codes{i}", align_bytes=64) for i in (Y, E, H)]
+        w_scales = [keep.tile([P, N], U8, name=f"w_scales{i}", align_bytes=64) for i in (Y, E, H)]
+        results = [[keep.tile([P, S], F32, name=f"result{i}_{b}") for b in range(BLOCKS)] for i in (Y, E, H)]
+        centre = [keep.tile([P, V], F32, name=f"centre{b}") for b in range(BLOCKS)]
+        total = [keep.tile([P, V], F32, name=f"total{b}") for b in range(BLOCKS)]
+        message = {(b, d): keep.tile([P, V], F32, name=f"message{b}_{d}") for b in range(BLOCKS) for d in range(NEIGHBOURS)}
+        turned = keep.tile([P, V], F32, name="turned")
+        shared = keep.tile([P, V + MID], F32, name="shared")
+        logit = {bd: keep.tile([P, V], F32, name=f"logit{bd[0]}_{bd[1]}") for bd in ((0, 0), (0, 1), (1, 0))}
+        logit[1, 1] = shared[:, :V]
+        gate = {bd: keep.tile([P, V], F32, name=f"gate{bd[0]}_{bd[1]}") for bd in ((0, 0), (1, 0), (1, 1))}
+        gate[0, 1] = shared[:, MID:]
+
+        def entries(list_tile, first, last):
+            return list_tile[:, first // STRIPE:last // STRIPE]
 
         def gather_x(j, u):
-            cols = slice(u * HALF // STRIPE, (u + 1) * HALF // STRIPE)
-            nc.vector.tensor_copy(grouped[u][:, :, j], planes[j][:].indirect(offs_t[:, cols]))
+            nc.vector.tensor_copy(grouped[u][:, :, j], planes[j][:].indirect(entries(offs_t, u * HALF, (u + 1) * HALF)))
 
         def quantize(codes, scales, values):
             nc.vector.quantize_mx(out=codes.bitcast(FP8X4), scales=scales, in_=values.rearrange("p c j -> p (c j)"))
@@ -84,112 +98,95 @@ def tile_picked_gatedg_none_e_kernel(tc, xT, w1, w2, w3, offs, cen, pos1, pos2, 
             u = first // HALF
             quantize(x_codes[:, first:last], x_scales[:, first:last], grouped[u][:, first - u * HALF:last - u * HALF, :])
 
-        def quantize_w(i, first=0, last=N):
-            quantize(w_codes[i][:, first:last], w_scales[i][:, first:last], w_grouped[i][:, first:last, :])
+        def quantize_w(i):
+            quantize(w_codes[i][:], w_scales[i][:], w_grouped[i][:])
 
-        def interleave_w(i, first=0, last=N):
-            nc.scalar.copy(w_grouped[i][:, first:last, :].rearrange("p (c n) j -> p c j n", n=4),
-                           w_raw[i][:, :, first:last].rearrange("p j (c n) -> p c j n", n=4))
+        def interleave_w(i):
+            nc.scalar.copy(w_grouped[i][:].rearrange("p (c n) j -> p c j n", n=RUN),
+                           w_raw[i][:].rearrange("p j (c n) -> p c j n", n=RUN))
 
-        def product(i, b, first, last, on_vector=False):
-            acc = psum.tile([P, HALF], F32, name="acc")
+        def product(i, b, first, last, copy_out):
+            acc = psum.tile([P, BANK], F32, name="acc")
             rows = slice(b * P, (b + 1) * P)
-            nc.tensor.matmul_mx(out=acc[:, :last - first], lhsT=w_codes[i][:, rows].bitcast(FP8X4), lhsT_scale=w_scales[i][:, rows],
-                                rhs=x_codes[:, first:last].bitcast(FP8X4), rhs_scale=x_scales[:, first:last], start=True, stop=True)
-            dst = res[i][b][:, first:last]
-            if on_vector:
-                nc.vector.tensor_copy(dst, acc[:, :last - first])
-            else:
-                nc.scalar.copy(dst, acc[:, :last - first])
+            nc.tensor.matmul_mx(out=acc[:, :last - first],
+                                lhsT=w_codes[i][:, rows].bitcast(FP8X4), lhsT_scale=w_scales[i][:, rows],
+                                rhs=x_codes[:, first:last].bitcast(FP8X4), rhs_scale=x_scales[:, first:last],
+                                start=True, stop=True)
+            copy_out(results[i][b][:, first:last], acc[:, :last - first])
 
-        def tiles(stem):
-            return [[keep.tile([P, V], F32, name=f"{stem}{b}_{d}") for d in range(2)] for b in range(BLOCKS)]
+        def whole_product(i, b):
+            for first in range(0, S, BANK):
+                product(i, b, first, first + BANK, nc.scalar.copy)
 
-        yc = [keep.tile([P, V], F32, name=f"yc{b}") for b in range(BLOCKS)]
-        z = [keep.tile([P, V], F32, name=f"z{b}") for b in range(BLOCKS)]
-        pre, gate, msg = tiles("pre"), tiles("gate"), tiles("msg")
+        def make_gate(b, d):
+            nc.vector.tensor_tensor(logit[b, d][:], results[E][b][:].indirect(pos_t[d][:]), centre[b][:], ADD)
+            nc.scalar.activation(gate[b, d][:], logit[b, d][:], SIGMOID)
 
-        def message(b, d, first=0, last=V):
-            nc.vector.tensor_tensor(msg[b][d][:, first:last], res[2][b][:].indirect(pos_t[d][:, first // STRIPE:last // STRIPE]),
-                                    gate[b][d][:, first:last], MULT)
-
-        def finish(b, queue, first=0, last=V):
-            nc.vector.tensor_tensor(z[b][:, first:last], msg[b][0][:, first:last], msg[b][1][:, first:last], ADD)
-            queue.dma_start(out=out[b * P:(b + 1) * P, first:last], in_=z[b][:, first:last])
-
-        turned_sb = keep.tile([P, V], F32, name="turned_sb")
+        def make_message(b, d, first, last):
+            nc.vector.tensor_tensor(message[b, d][:, first:last], results[H][b][:].indirect(entries(pos_t[d], first, last)),
+                                    gate[b, d][:, first:last], MULT)
 
         def add_turned(b, first, last):
             squares = [slice(c, c + P) for c in range(first, last, P)]
-            turned = psum.tile([P, HALF], F32, name="acc")
-            for d in range(2):
+            acc = psum.tile([P, BANK], F32, name="acc")
+            for d in range(NEIGHBOURS):
                 for c, cols in enumerate(squares):
-                    nc.tensor.matmul(turned[:, cols], msg[b][d][:, cols], identity[:], is_transpose=True,
-                                     start=(d == 0 and c == 0), stop=(d == 1 and c == len(squares) - 1))
-            nc.scalar.copy(turned_sb[:, first:last], turned[:, first:last])
+                    nc.tensor.matmul(acc[:, cols], message[b, d][:, cols], identity[:], is_transpose=True,
+                                     start=(d == 0 and c == 0), stop=(d == NEIGHBOURS - 1 and c == len(squares) - 1))
+            nc.scalar.copy(turned[:, first:last], acc[:, first:last])
 
-        def turn_back(b, first, last):
-            back = psum.tile([P, HALF], F32, name="acc")
-            for c in range(first, last, P):
-                nc.tensor.transpose(back[:, c:c + P], turned_sb[:, c:c + P], identity[:])
-            nc.scalar.copy(z[b][:, first:last], back[:, first:last])
-            nc.scalar.dma_start(out=out[b * P:(b + 1) * P, first:last], in_=z[b][:, first:last])
+        def turn_back_and_store(b):
+            acc = psum.tile([P, BANK], F32, name="acc")
+            for c in range(0, V, P):
+                nc.tensor.transpose(acc[:, c:c + P], turned[:, c:c + P], identity[:])
+            nc.scalar.copy(total[b][:], acc[:])
+            nc.scalar.dma_start(out=out[b * P:(b + 1) * P, :], in_=total[b][:])
 
-        def centre(b):
-            nc.vector.tensor_copy(yc[b][:], res[0][b][:].indirect(cen_t[:]))
+        def add_and_store(b, first, last):
+            nc.vector.tensor_tensor(total[b][:, first:last], message[b, 0][:, first:last], message[b, 1][:, first:last], ADD)
+            nc.sync.dma_start(out=out[b * P:(b + 1) * P, first:last], in_=total[b][:, first:last])
 
-        def gating(b, d):
-            nc.vector.tensor_tensor(pre[b][d][:], res[1][b][:].indirect(pos_t[d][:]), yc[b][:], ADD)
-            nc.scalar.activation(gate[b][d][:], pre[b][d][:], SIGMOID)
-
-        def both(i, b):
-            for u in range(HALVES):
-                product(i, b, u * HALF, (u + 1) * HALF)
-
-        for j in range(PACK - 1):
-            for u in range(HALVES):
+        for j in range(LAST):
+            for u in range(S // HALF):
                 gather_x(j, u)
-        interleave_w(0)
-        quantize_w(0)
-        for c, (first, last) in enumerate(CHUNKS):
-            if c in (2, 3,):
-                nc.vector.tensor_copy(rounded[:, first:last], planes[PACK - 1][:, first:last])
-            else:
-                nc.scalar.copy(rounded[:, first:last], planes[PACK - 1][:, first:last])
-        gather_x(PACK - 1, 0)
-        nc.scalar.activation(grouped[1][:, :, PACK - 1], rounded[:].indirect(offs_t[:, HALF // STRIPE:]), COPY)
-        quantize_x(0, 512)
-        interleave_w(1)
-        interleave_w(2)
-        quantize_x(512, 768)
-        quantize_x(768, 1024)
-        product(0, 0, 0, 512, True)
-        quantize_w(1)
-        product(0, 0, 512, 768, True)
-        product(0, 0, 768, 1024, True)
-        quantize_w(2)
-        both(0, 1)
-        both(1, 0)
-        both(1, 1)
-        both(2, 0)
-        centre(0)
-        centre(1)
-        shared = keep.tile([P, V + V // 2], F32, name="shared")
-        gate[0][1] = shared[:, V // 2:]
-        pre[1][1] = shared[:, :V]
-        gating(0, 0)
-        gating(0, 1)
-        both(2, 1)
-        gating(1, 0)
-        message(0, 0)
-        message(0, 1, 0, 256)
-        message(0, 1, 256, 512)
-        add_turned(0, 0, 256)
-        add_turned(0, 256, 512)
-        gating(1, 1)
-        turn_back(0, 0, 512)
-        message(1, 0)
-        message(1, 1, 0, 256)
-        message(1, 1, 256, 512)
-        finish(1, nc.sync, 0, 256)
-        finish(1, nc.sync, 256, 512)
+        interleave_w(Y)
+        quantize_w(Y)
+        for first, last, on_vector in CHUNKS:
+            round_chunk = nc.vector.tensor_copy if on_vector else nc.scalar.copy
+            round_chunk(rounded[:, first:last], planes[LAST][:, first:last])
+        gather_x(LAST, 0)
+        nc.scalar.activation(grouped[1][:, :, LAST], rounded[:].indirect(entries(offs_t, HALF, S)), COPY)
+
+        quantize_x(0, HALF)
+        interleave_w(E)
+        interleave_w(H)
+        quantize_x(HALF, HALF + QUARTER)
+        quantize_x(HALF + QUARTER, S)
+        product(Y, 0, 0, HALF, nc.vector.tensor_copy)
+        quantize_w(E)
+        product(Y, 0, HALF, HALF + QUARTER, nc.vector.tensor_copy)
+        product(Y, 0, HALF + QUARTER, S, nc.vector.tensor_copy)
+        quantize_w(H)
+        whole_product(Y, 1)
+        for b in range(BLOCKS):
+            whole_product(E, b)
+        whole_product(H, 0)
+
+        for b in range(BLOCKS):
+            nc.vector.tensor_copy(centre[b][:], results[Y][b][:].indirect(cen_t[:]))
+        for d in range(NEIGHBOURS):
+            make_gate(0, d)
+        whole_product(H, 1)
+        make_gate(1, 0)
+        make_message(0, 0, 0, V)
+        for first in (0, MID):
+            make_message(0, 1, first, first + MID)
+        for first in (0, MID):
+            add_turned(0, first, first + MID)
+        make_gate(1, 1)
+        turn_back_and_store(0)
+        make_message(1, 0, 0, V)
+        for first in (0, MID):
+            make_message(1, 1, first, first + MID)
+        for first in (0, MID):
+            add_and_store(1, first, first + MID)

@@ -41,6 +41,11 @@ def tile_picked_gatedg_none_e_kernel(tc, xT, w1, w2, w3, offs, cen, pos1, pos2, 
         keep = ctx.enter_context(tc.tile_pool(name="keep", bufs=1))
         psum = ctx.enter_context(tc.psum_pool(name="psum", bufs=BANKS))
 
+        warm_in = keep.tile([P, 1], F32, name="warm_in")
+        warm_out = keep.tile([P, 1], F32, name="warm_out")
+        nc.vector.memset(warm_in[:], 0.0)
+        nc.scalar.activation(warm_out[:], warm_in[:], SIGMOID)
+
         identity = keep.tile([P, P], F32, name="identity")
         make_identity(nc, identity[:])
 
@@ -79,11 +84,8 @@ def tile_picked_gatedg_none_e_kernel(tc, xT, w1, w2, w3, offs, cen, pos1, pos2, 
         total = [keep.tile([P, V], F32, name=f"total{b}") for b in range(BLOCKS)]
         message = {(b, d): keep.tile([P, V], F32, name=f"message{b}_{d}") for b in range(BLOCKS) for d in range(NEIGHBOURS)}
         turned = keep.tile([P, V], F32, name="turned")
-        shared = keep.tile([P, V + MID], F32, name="shared")
-        logit = {bd: keep.tile([P, V], F32, name=f"logit{bd[0]}_{bd[1]}") for bd in ((0, 0), (0, 1), (1, 0))}
-        logit[1, 1] = shared[:, :V]
-        gate = {bd: keep.tile([P, V], F32, name=f"gate{bd[0]}_{bd[1]}") for bd in ((0, 0), (1, 0), (1, 1))}
-        gate[0, 1] = shared[:, MID:]
+        logit = {(b, d): keep.tile([P, V], F32, name=f"logit{b}_{d}") for b in range(BLOCKS) for d in range(NEIGHBOURS)}
+        gate = {(b, d): keep.tile([P, V], F32, name=f"gate{b}_{d}") for b in range(BLOCKS) for d in range(NEIGHBOURS)}
 
         def entries(list_tile, first, last):
             return list_tile[:, first // STRIPE:last // STRIPE]
@@ -135,12 +137,12 @@ def tile_picked_gatedg_none_e_kernel(tc, xT, w1, w2, w3, offs, cen, pos1, pos2, 
                                      start=(d == 0 and c == 0), stop=(d == NEIGHBOURS - 1 and c == len(squares) - 1))
             nc.scalar.copy(turned[:, first:last], acc[:, first:last])
 
-        def turn_back_and_store(b):
+        def turn_back_and_store(b, first, last):
             acc = psum.tile([P, BANK], F32, name="acc")
-            for c in range(0, V, P):
+            for c in range(first, last, P):
                 nc.tensor.transpose(acc[:, c:c + P], turned[:, c:c + P], identity[:])
-            nc.scalar.copy(total[b][:], acc[:])
-            nc.scalar.dma_start(out=out[b * P:(b + 1) * P, :], in_=total[b][:])
+            nc.scalar.copy(total[b][:, first:last], acc[:, first:last])
+            nc.scalar.dma_start(out=out[b * P:(b + 1) * P, first:last], in_=total[b][:, first:last])
 
         def add_and_store(b, first, last):
             nc.vector.tensor_tensor(total[b][:, first:last], message[b, 0][:, first:last], message[b, 1][:, first:last], ADD)
@@ -159,32 +161,34 @@ def tile_picked_gatedg_none_e_kernel(tc, xT, w1, w2, w3, offs, cen, pos1, pos2, 
 
         quantize_x(0, HALF)
         interleave_w(E)
-        interleave_w(H)
         quantize_x(HALF, HALF + QUARTER)
         quantize_x(HALF + QUARTER, S)
-        product(Y, 0, 0, HALF, nc.vector.tensor_copy)
-        quantize_w(E)
+        product(Y, 0, 0, HALF, nc.scalar.copy)
         product(Y, 0, HALF, HALF + QUARTER, nc.vector.tensor_copy)
         product(Y, 0, HALF + QUARTER, S, nc.vector.tensor_copy)
-        quantize_w(H)
+        quantize_w(E)
         whole_product(Y, 1)
-        for b in range(BLOCKS):
-            whole_product(E, b)
-        whole_product(H, 0)
+        whole_product(E, 0)
+        interleave_w(H)
+        whole_product(E, 1)
 
         for b in range(BLOCKS):
             nc.vector.tensor_copy(centre[b][:], results[Y][b][:].indirect(cen_t[:]))
         for d in range(NEIGHBOURS):
             make_gate(0, d)
-        whole_product(H, 1)
-        make_gate(1, 0)
+        quantize_w(H)
+        for b in range(BLOCKS):
+            whole_product(H, b)
+        for d in range(NEIGHBOURS):
+            make_gate(1, d)
+
         make_message(0, 0, 0, V)
         for first in (0, MID):
             make_message(0, 1, first, first + MID)
         for first in (0, MID):
             add_turned(0, first, first + MID)
-        make_gate(1, 1)
-        turn_back_and_store(0)
+        for first in (0, MID):
+            turn_back_and_store(0, first, first + MID)
         make_message(1, 0, 0, V)
         for first in (0, MID):
             make_message(1, 1, first, first + MID)

@@ -26,16 +26,16 @@ BANKS = 8
 HALF = S // 2
 QUARTER = S // 4
 MID = V // 2
-BLOCKS = N // P
+BANDS = N // P
 NEIGHBOURS = 2
 Y, E, H = 0, 1, 2
 RUN = 4
-
-CHUNKS = ((0, 1024, False), (1024, 2048, False), (2048, 3072, True), (3072, 3712, True), (3712, T, False))
+CHUNKS = ((0, 2048, False), (2048, 3328, True), (3328, 3840, True), (3840, T, False))
 
 
 def tile_picked_gatedg_none_e_kernel(tc, xT, w1, w2, w3, offs, cen, pos1, pos2, out):
     nc = tc.nc
+    weights = (w1, w2, w3)
     with ExitStack() as ctx:
         lists = ctx.enter_context(tc.tile_pool(name="lists", bufs=1))
         keep = ctx.enter_context(tc.tile_pool(name="keep", bufs=1))
@@ -53,39 +53,42 @@ def tile_picked_gatedg_none_e_kernel(tc, xT, w1, w2, w3, offs, cen, pos1, pos2, 
         cen_t = lists.tile([P, V // STRIPE], U16, name="cen_t")
         pos_t = [lists.tile([P, V // STRIPE], U16, name=f"pos_t{d}") for d in range(NEIGHBOURS)]
         planes = [keep.tile([P, T], F32, name=f"plane{j}") for j in range(PACK)]
-        w_raw = [keep.tile([P, PACK, N], F32, name=f"w_raw{i}") for i in (Y, E, H)]
+        w_raw = {(i, b): keep.tile([P, PACK, P], F32, name=f"w_raw{i}_{b}", tag=f"w_raw{i}_{b}", align_bytes=64)
+                 for i in (Y, E, H) for b in range(BANDS)}
         x_rows = xT.rearrange("(p j) t -> p j t", j=PACK)
 
-        def load_w(i, w):
-            nc.sync.dma_start(out=w_raw[i][:], in_=w.rearrange("(p j) n -> p j n", j=PACK))
+        def load_w(i, b):
+            nc.sync.dma_start(out=w_raw[i, b][:], in_=weights[i].rearrange("(p j) n -> p j n", j=PACK)[:, :, b * P:(b + 1) * P])
 
         nc.sync.dma_start(out=planes[0][:], in_=x_rows[:, 0, :])
         nc.sync.dma_start(offs_t[:], offs)
         for j in range(1, LAST):
             nc.sync.dma_start(out=planes[j][:], in_=x_rows[:, j, :])
-        load_w(Y, w1)
         for first, last, on_vector in CHUNKS:
             nc.sync.dma_start(out=planes[LAST][:, first:last], in_=x_rows[:, LAST, first:last])
-        load_w(E, w2)
+        for i in (Y, E, H):
+            load_w(i, 0)
         nc.sync.dma_start(cen_t[:], cen)
         nc.sync.dma_start(pos_t[0][:], pos1)
-        load_w(H, w3)
         nc.sync.dma_start(pos_t[1][:], pos2)
+        for i in (Y, E, H):
+            load_w(i, 1)
 
         rounded = keep.tile([P, T], BF16, name="rounded")
         grouped = [keep.tile([P, HALF, PACK], BF16, name=f"grouped{u}", align_bytes=64) for u in range(S // HALF)]
-        x_codes = keep.tile([P, S], U32, name="x_codes", align_bytes=64)
+        x_codes = {}
         x_scales = keep.tile([P, S], U8, name="x_scales", align_bytes=64)
-        w_grouped = [keep.tile([P, N, PACK], BF16, name=f"w_grouped{i}", align_bytes=64) for i in (Y, E, H)]
-        w_codes = [keep.tile([P, N], U32, name=f"w_codes{i}", align_bytes=64) for i in (Y, E, H)]
-        w_scales = [keep.tile([P, N], U8, name=f"w_scales{i}", align_bytes=64) for i in (Y, E, H)]
-        results = [[keep.tile([P, S], F32, name=f"result{i}_{b}") for b in range(BLOCKS)] for i in (Y, E, H)]
-        centre = [keep.tile([P, V], F32, name=f"centre{b}") for b in range(BLOCKS)]
-        total = [keep.tile([P, V], F32, name=f"total{b}") for b in range(BLOCKS)]
-        message = {(b, d): keep.tile([P, V], F32, name=f"message{b}_{d}") for b in range(BLOCKS) for d in range(NEIGHBOURS)}
+        w_grouped = {key: keep.tile([P, P, PACK], BF16, name=f"w_grouped{key[0]}_{key[1]}", align_bytes=64) for key in w_raw}
+        w_codes = {key: keep.tile([P, P], U32, name=f"w_codes{key[0]}_{key[1]}", align_bytes=64) for key in w_raw}
+        w_scales = {key: keep.tile([P, P], U8, name=f"w_scales{key[0]}_{key[1]}", align_bytes=64) for key in w_raw}
+        results = {key: keep.tile([P, S], F32, name=f"result{key[0]}_{key[1]}") for key in w_raw}
+        centre = [keep.tile([P, V], F32, name=f"centre{b}") for b in range(BANDS)]
+        total = [keep.tile([P, V], F32, name=f"total{b}") for b in range(BANDS)]
+        edges = [(b, d) for b in range(BANDS) for d in range(NEIGHBOURS)]
+        message = {(b, d): keep.tile([P, V], F32, name=f"message{b}_{d}") for b, d in edges}
+        logit = {(b, d): keep.tile([P, V], F32, name=f"logit{b}_{d}") for b, d in edges}
+        gate = {(b, d): keep.tile([P, V], F32, name=f"gate{b}_{d}") for b, d in edges}
         turned = keep.tile([P, V], F32, name="turned")
-        logit = {(b, d): keep.tile([P, V], F32, name=f"logit{b}_{d}") for b in range(BLOCKS) for d in range(NEIGHBOURS)}
-        gate = {(b, d): keep.tile([P, V], F32, name=f"gate{b}_{d}") for b in range(BLOCKS) for d in range(NEIGHBOURS)}
 
         def entries(list_tile, first, last):
             return list_tile[:, first // STRIPE:last // STRIPE]
@@ -98,34 +101,39 @@ def tile_picked_gatedg_none_e_kernel(tc, xT, w1, w2, w3, offs, cen, pos1, pos2, 
 
         def quantize_x(first, last):
             u = first // HALF
-            quantize(x_codes[:, first:last], x_scales[:, first:last], grouped[u][:, first - u * HALF:last - u * HALF, :])
+            quantize(x_codes[u][:, first - u * HALF:last - u * HALF], x_scales[:, first:last], grouped[u][:, first - u * HALF:last - u * HALF, :])
 
-        def quantize_w(i):
-            quantize(w_codes[i][:], w_scales[i][:], w_grouped[i][:])
+        def quantize_w(i, b):
+            quantize(w_codes[i, b][:], w_scales[i, b][:], w_grouped[i, b][:])
 
-        def interleave_w(i):
-            nc.scalar.copy(w_grouped[i][:].rearrange("p (c n) j -> p c j n", n=RUN),
-                           w_raw[i][:].rearrange("p j (c n) -> p c j n", n=RUN))
+        def interleave_w(i, b, copy):
+            copy(w_grouped[i, b][:].rearrange("p (c n) j -> p c j n", n=RUN),
+                 w_raw[i, b][:].rearrange("p j (c n) -> p c j n", n=RUN))
 
         def product(i, b, first, last, copy_out):
             acc = psum.tile([P, BANK], F32, name="acc")
-            rows = slice(b * P, (b + 1) * P)
+            u = first // HALF
             nc.tensor.matmul_mx(out=acc[:, :last - first],
-                                lhsT=w_codes[i][:, rows].bitcast(FP8X4), lhsT_scale=w_scales[i][:, rows],
-                                rhs=x_codes[:, first:last].bitcast(FP8X4), rhs_scale=x_scales[:, first:last],
+                                lhsT=w_codes[i, b][:].bitcast(FP8X4), lhsT_scale=w_scales[i, b][:],
+                                rhs=x_codes[u][:, first - u * HALF:last - u * HALF].bitcast(FP8X4), rhs_scale=x_scales[:, first:last],
                                 start=True, stop=True)
-            copy_out(results[i][b][:, first:last], acc[:, :last - first])
+            copy_out(results[i, b][:, first:last], acc[:, :last - first])
 
         def whole_product(i, b):
             for first in range(0, S, BANK):
                 product(i, b, first, first + BANK, nc.scalar.copy)
 
+        def fetch_centre(b):
+            nc.vector.tensor_copy(centre[b][:], results[Y, b][:].indirect(cen_t[:]))
+
+        def make_logit(b, d):
+            nc.vector.tensor_tensor(logit[b, d][:], results[E, b][:].indirect(pos_t[d][:]), centre[b][:], ADD)
+
         def make_gate(b, d):
-            nc.vector.tensor_tensor(logit[b, d][:], results[E][b][:].indirect(pos_t[d][:]), centre[b][:], ADD)
             nc.scalar.activation(gate[b, d][:], logit[b, d][:], SIGMOID)
 
         def make_message(b, d, first, last):
-            nc.vector.tensor_tensor(message[b, d][:, first:last], results[H][b][:].indirect(entries(pos_t[d], first, last)),
+            nc.vector.tensor_tensor(message[b, d][:, first:last], results[H, b][:].indirect(entries(pos_t[d], first, last)),
                                     gate[b, d][:, first:last], MULT)
 
         def add_turned(b, first, last):
@@ -142,7 +150,7 @@ def tile_picked_gatedg_none_e_kernel(tc, xT, w1, w2, w3, offs, cen, pos1, pos2, 
             for c in range(first, last, P):
                 nc.tensor.transpose(acc[:, c:c + P], turned[:, c:c + P], identity[:])
             nc.scalar.copy(total[b][:, first:last], acc[:, first:last])
-            nc.scalar.dma_start(out=out[b * P:(b + 1) * P, first:last], in_=total[b][:, first:last])
+            nc.sync.dma_start(out=out[b * P:(b + 1) * P, first:last], in_=total[b][:, first:last])
 
         def add_and_store(b, first, last):
             nc.vector.tensor_tensor(total[b][:, first:last], message[b, 0][:, first:last], message[b, 1][:, first:last], ADD)
@@ -151,44 +159,51 @@ def tile_picked_gatedg_none_e_kernel(tc, xT, w1, w2, w3, offs, cen, pos1, pos2, 
         for j in range(LAST):
             for u in range(S // HALF):
                 gather_x(j, u)
-        interleave_w(Y)
-        quantize_w(Y)
         for first, last, on_vector in CHUNKS:
             round_chunk = nc.vector.tensor_copy if on_vector else nc.scalar.copy
             round_chunk(rounded[:, first:last], planes[LAST][:, first:last])
         gather_x(LAST, 0)
         nc.scalar.activation(grouped[1][:, :, LAST], rounded[:].indirect(entries(offs_t, HALF, S)), COPY)
 
+        interleave_w(Y, 0, nc.vector.tensor_copy)
+        x_codes[0] = keep.tile([P, HALF], U32, name="x_codes0", tag=f"w_raw{Y}_0", align_bytes=64)
+        x_codes[1] = keep.tile([P, HALF], U32, name="x_codes1", align_bytes=64)
         quantize_x(0, HALF)
-        interleave_w(E)
+        quantize_w(Y, 0)
         quantize_x(HALF, HALF + QUARTER)
         quantize_x(HALF + QUARTER, S)
+        interleave_w(E, 0, nc.scalar.copy)
+        interleave_w(H, 0, nc.scalar.copy)
+        quantize_w(E, 0)
+        quantize_w(H, 0)
         product(Y, 0, 0, HALF, nc.scalar.copy)
         product(Y, 0, HALF, HALF + QUARTER, nc.vector.tensor_copy)
         product(Y, 0, HALF + QUARTER, S, nc.vector.tensor_copy)
-        quantize_w(E)
-        whole_product(Y, 1)
         whole_product(E, 0)
-        interleave_w(H)
-        whole_product(E, 1)
-
-        for b in range(BLOCKS):
-            nc.vector.tensor_copy(centre[b][:], results[Y][b][:].indirect(cen_t[:]))
-        for d in range(NEIGHBOURS):
-            make_gate(0, d)
-        quantize_w(H)
-        for b in range(BLOCKS):
-            whole_product(H, b)
-        for d in range(NEIGHBOURS):
-            make_gate(1, d)
-
+        fetch_centre(0)
+        whole_product(H, 0)
+        make_logit(0, 0)
+        make_logit(0, 1)
+        interleave_w(Y, 1, nc.scalar.copy)
+        make_gate(0, 0)
+        interleave_w(E, 1, nc.scalar.copy)
+        make_gate(0, 1)
+        quantize_w(Y, 1)
         make_message(0, 0, 0, V)
-        for first in (0, MID):
-            make_message(0, 1, first, first + MID)
-        for first in (0, MID):
-            add_turned(0, first, first + MID)
-        for first in (0, MID):
-            turn_back_and_store(0, first, first + MID)
+        quantize_w(E, 1)
+        make_message(0, 1, 0, V)
+        whole_product(Y, 1)
+        interleave_w(H, 1, nc.scalar.copy)
+        whole_product(E, 1)
+        fetch_centre(1)
+        quantize_w(H, 1)
+        make_logit(1, 0)
+        make_logit(1, 1)
+        add_turned(0, 0, V)
+        whole_product(H, 1)
+        make_gate(1, 0)
+        turn_back_and_store(0, 0, V)
+        make_gate(1, 1)
         make_message(1, 0, 0, V)
         for first in (0, MID):
             make_message(1, 1, first, first + MID)

@@ -35,7 +35,6 @@ CHUNKS = ((0, 2048, False), (2048, 3328, True), (3328, 3840, True), (3840, T, Fa
 
 def tile_picked_gatedg_none_e_kernel(tc, xT, w1, w2, w3, offs, cen, pos1, pos2, out):
     nc = tc.nc
-    weights = (w1, w2, w3)
     with ExitStack() as ctx:
         lists = ctx.enter_context(tc.tile_pool(name="lists", bufs=1))
         keep = ctx.enter_context(tc.tile_pool(name="keep", bufs=1))
@@ -53,12 +52,17 @@ def tile_picked_gatedg_none_e_kernel(tc, xT, w1, w2, w3, offs, cen, pos1, pos2, 
         cen_t = lists.tile([P, V // STRIPE], U16, name="cen_t")
         pos_t = [lists.tile([P, V // STRIPE], U16, name=f"pos_t{d}") for d in range(NEIGHBOURS)]
         planes = [keep.tile([P, T], F32, name=f"plane{j}") for j in range(PACK)]
-        w_raw = {(i, b): keep.tile([P, PACK, P], F32, name=f"w_raw{i}_{b}", tag=f"w_raw{i}_{b}", align_bytes=64)
-                 for i in (Y, E, H) for b in range(BANDS)}
+        w1_raw = [keep.tile([P, PACK, P], F32, name=f"w1_raw{b}") for b in range(BANDS)]
+        w2_raw = [keep.tile([P, PACK, P], F32, name=f"w2_raw{b}") for b in range(BANDS)]
+        w3_raw = keep.tile([P, PACK, N], F32, name="w3_raw")
+        w_raw = {(Y, b): w1_raw[b][:] for b in range(BANDS)}
+        for b in range(BANDS):
+            w_raw[E, b] = w2_raw[b][:]
+            w_raw[H, b] = w3_raw[:, :, b * P:(b + 1) * P]
         x_rows = xT.rearrange("(p j) t -> p j t", j=PACK)
 
-        def load_w(i, b):
-            nc.sync.dma_start(out=w_raw[i, b][:], in_=weights[i].rearrange("(p j) n -> p j n", j=PACK)[:, :, b * P:(b + 1) * P])
+        def k_rows(w):
+            return w.rearrange("(p j) n -> p j n", j=PACK)
 
         nc.sync.dma_start(out=planes[0][:], in_=x_rows[:, 0, :])
         nc.sync.dma_start(offs_t[:], offs)
@@ -66,22 +70,42 @@ def tile_picked_gatedg_none_e_kernel(tc, xT, w1, w2, w3, offs, cen, pos1, pos2, 
             nc.sync.dma_start(out=planes[j][:], in_=x_rows[:, j, :])
         for first, last, on_vector in CHUNKS:
             nc.sync.dma_start(out=planes[LAST][:, first:last], in_=x_rows[:, LAST, first:last])
-        for i in (Y, E, H):
-            load_w(i, 0)
+        for b in range(BANDS):
+            nc.sync.dma_start(out=w1_raw[b][:], in_=k_rows(w1)[:, :, b * P:(b + 1) * P])
+        nc.sync.dma_start(out=w2_raw[0][:], in_=k_rows(w2)[:, :, :P])
         nc.sync.dma_start(cen_t[:], cen)
+        nc.sync.dma_start(out=w2_raw[1][:], in_=k_rows(w2)[:, :, P:])
+        nc.sync.dma_start(out=w3_raw[:], in_=k_rows(w3))
         nc.sync.dma_start(pos_t[0][:], pos1)
         nc.sync.dma_start(pos_t[1][:], pos2)
-        for i in (Y, E, H):
-            load_w(i, 1)
 
         rounded = keep.tile([P, T], BF16, name="rounded")
         grouped = [keep.tile([P, HALF, PACK], BF16, name=f"grouped{u}", align_bytes=64) for u in range(S // HALF)]
-        x_codes = {}
+        x_codes = [keep.tile([P, HALF], U32, name=f"x_codes{u}", align_bytes=64) for u in range(S // HALF)]
         x_scales = keep.tile([P, S], U8, name="x_scales", align_bytes=64)
-        w_grouped = {key: keep.tile([P, P, PACK], BF16, name=f"w_grouped{key[0]}_{key[1]}", align_bytes=64) for key in w_raw}
-        w_codes = {key: keep.tile([P, P], U32, name=f"w_codes{key[0]}_{key[1]}", align_bytes=64) for key in w_raw}
-        w_scales = {key: keep.tile([P, P], U8, name=f"w_scales{key[0]}_{key[1]}", align_bytes=64) for key in w_raw}
-        results = {key: keep.tile([P, S], F32, name=f"result{key[0]}_{key[1]}") for key in w_raw}
+        w_grouped, w_codes, w_scales, results = {}, {}, {}, {}
+        for i in (Y, E, H):
+            for b in range(BANDS):
+                results[i, b] = keep.tile([P, S], F32, name=f"result{i}_{b}", tag=f"result{i}_{b}", align_bytes=64)
+
+        def weight_tiles(keys, grouped_tag):
+            width = len(keys) * P
+            name = f"{keys[0][0]}_{keys[0][1]}"
+            values = keep.tile([P, width, PACK], BF16, name=f"w_grouped{name}", tag=grouped_tag, align_bytes=64)
+            for n, key in enumerate(keys):
+                w_grouped[key] = values[:, n * P:(n + 1) * P, :]
+            return values
+
+        def quantize_w(keys, values, codes_tag):
+            width = len(keys) * P
+            name = f"{keys[0][0]}_{keys[0][1]}"
+            codes = keep.tile([P, width], U32, name=f"w_codes{name}", tag=codes_tag, align_bytes=64)
+            scales = keep.tile([P, width], U8, name=f"w_scales{name}", align_bytes=64)
+            for n, key in enumerate(keys):
+                w_codes[key] = codes[:, n * P:(n + 1) * P]
+                w_scales[key] = scales[:, n * P:(n + 1) * P]
+            quantize(codes[:], scales[:], values[:])
+
         centre = [keep.tile([P, V], F32, name=f"centre{b}") for b in range(BANDS)]
         total = [keep.tile([P, V], F32, name=f"total{b}") for b in range(BANDS)]
         edges = [(b, d) for b in range(BANDS) for d in range(NEIGHBOURS)]
@@ -103,18 +127,18 @@ def tile_picked_gatedg_none_e_kernel(tc, xT, w1, w2, w3, offs, cen, pos1, pos2, 
             u = first // HALF
             quantize(x_codes[u][:, first - u * HALF:last - u * HALF], x_scales[:, first:last], grouped[u][:, first - u * HALF:last - u * HALF, :])
 
-        def quantize_w(i, b):
-            quantize(w_codes[i, b][:], w_scales[i, b][:], w_grouped[i, b][:])
+        def interleave_w_on_gpsimd(i, b):
+            nc.gpsimd.tensor_scalar(w_grouped[i, b], w_raw[i, b].rearrange("p j n -> p n j"), 1.0, 0.0, MULT, ADD)
 
         def interleave_w(i, b, copy):
-            copy(w_grouped[i, b][:].rearrange("p (c n) j -> p c j n", n=RUN),
-                 w_raw[i, b][:].rearrange("p j (c n) -> p c j n", n=RUN))
+            copy(w_grouped[i, b].rearrange("p (c n) j -> p c j n", n=RUN),
+                 w_raw[i, b].rearrange("p j (c n) -> p c j n", n=RUN))
 
         def product(i, b, first, last, copy_out):
             acc = psum.tile([P, BANK], F32, name="acc")
             u = first // HALF
             nc.tensor.matmul_mx(out=acc[:, :last - first],
-                                lhsT=w_codes[i, b][:].bitcast(FP8X4), lhsT_scale=w_scales[i, b][:],
+                                lhsT=w_codes[i, b].bitcast(FP8X4), lhsT_scale=w_scales[i, b],
                                 rhs=x_codes[u][:, first - u * HALF:last - u * HALF].bitcast(FP8X4), rhs_scale=x_scales[:, first:last],
                                 start=True, stop=True)
             copy_out(results[i, b][:, first:last], acc[:, :last - first])
@@ -150,7 +174,7 @@ def tile_picked_gatedg_none_e_kernel(tc, xT, w1, w2, w3, offs, cen, pos1, pos2, 
             for c in range(first, last, P):
                 nc.tensor.transpose(acc[:, c:c + P], turned[:, c:c + P], identity[:])
             nc.scalar.copy(total[b][:, first:last], acc[:, first:last])
-            nc.sync.dma_start(out=out[b * P:(b + 1) * P, first:last], in_=total[b][:, first:last])
+            nc.scalar.dma_start(out=out[b * P:(b + 1) * P, first:last], in_=total[b][:, first:last])
 
         def add_and_store(b, first, last):
             nc.vector.tensor_tensor(total[b][:, first:last], message[b, 0][:, first:last], message[b, 1][:, first:last], ADD)
@@ -165,45 +189,50 @@ def tile_picked_gatedg_none_e_kernel(tc, xT, w1, w2, w3, offs, cen, pos1, pos2, 
         gather_x(LAST, 0)
         nc.scalar.activation(grouped[1][:, :, LAST], rounded[:].indirect(entries(offs_t, HALF, S)), COPY)
 
-        interleave_w(Y, 0, nc.vector.tensor_copy)
-        x_codes[0] = keep.tile([P, HALF], U32, name="x_codes0", tag=f"w_raw{Y}_0", align_bytes=64)
-        x_codes[1] = keep.tile([P, HALF], U32, name="x_codes1", align_bytes=64)
+        y0 = weight_tiles([(Y, 0)], "values_y0")
+        y1 = weight_tiles([(Y, 1)], "values_y1")
+        e0 = weight_tiles([(E, 0)], "values_e")
+        interleave_w_on_gpsimd(Y, 0)
         quantize_x(0, HALF)
-        quantize_w(Y, 0)
+        quantize_w([(Y, 0)], y0, "codes_y0")
         quantize_x(HALF, HALF + QUARTER)
         quantize_x(HALF + QUARTER, S)
+        interleave_w(Y, 1, nc.scalar.copy)
         interleave_w(E, 0, nc.scalar.copy)
-        interleave_w(H, 0, nc.scalar.copy)
-        quantize_w(E, 0)
-        quantize_w(H, 0)
+        quantize_w([(Y, 1)], y1, "codes_y1")
         product(Y, 0, 0, HALF, nc.scalar.copy)
         product(Y, 0, HALF, HALF + QUARTER, nc.vector.tensor_copy)
         product(Y, 0, HALF + QUARTER, S, nc.vector.tensor_copy)
-        whole_product(E, 0)
-        fetch_centre(0)
-        whole_product(H, 0)
-        make_logit(0, 0)
-        make_logit(0, 1)
-        interleave_w(Y, 1, nc.scalar.copy)
-        make_gate(0, 0)
-        interleave_w(E, 1, nc.scalar.copy)
-        make_gate(0, 1)
-        quantize_w(Y, 1)
-        make_message(0, 0, 0, V)
-        quantize_w(E, 1)
-        make_message(0, 1, 0, V)
+        quantize_w([(E, 0)], e0, "codes_y0")
         whole_product(Y, 1)
-        interleave_w(H, 1, nc.scalar.copy)
-        whole_product(E, 1)
+        whole_product(E, 0)
+        late = weight_tiles([(E, 1), (H, 0)], "values_e")
+        interleave_w_on_gpsimd(E, 1)
+        interleave_w_on_gpsimd(H, 0)
+        fetch_centre(0)
         fetch_centre(1)
-        quantize_w(H, 1)
+        quantize_w([(E, 1), (H, 0)], late, f"result{Y}_1")
+        h1 = weight_tiles([(H, 1)], "values_h1")
+        interleave_w(H, 1, nc.scalar.copy)
+        make_logit(0, 0)
+        quantize_w([(H, 1)], h1, "codes_h1")
+        make_logit(0, 1)
+        whole_product(E, 1)
+        make_gate(0, 0)
+        make_gate(0, 1)
         make_logit(1, 0)
         make_logit(1, 1)
-        add_turned(0, 0, V)
-        whole_product(H, 1)
+        whole_product(H, 0)
         make_gate(1, 0)
-        turn_back_and_store(0, 0, V)
+        whole_product(H, 1)
         make_gate(1, 1)
+        make_message(0, 0, 0, V)
+        for first in (0, MID):
+            make_message(0, 1, first, first + MID)
+        for first in (0, MID):
+            add_turned(0, first, first + MID)
+        for first in (0, MID):
+            turn_back_and_store(0, first, first + MID)
         make_message(1, 0, 0, V)
         for first in (0, MID):
             make_message(1, 1, first, first + MID)

@@ -196,13 +196,16 @@ def tile_picked_gatedg_none_e_kernel(tc, xT, w1, w2, w3, offs, cen, pos1, pos2, 
         quantize_x(0, HALF)
         quantize_w([(Y, 0)], y0, "codes_y0")
         quantize_x(HALF, HALF + QUARTER)
-        quantize_x(HALF + QUARTER, S)
+        quantize_x(HALF + QUARTER, S - P)
+        quantize_x(S - P, S)
         interleave_w(Y, 1, nc.scalar.copy)
         interleave_w(E, 0, nc.scalar.copy)
         quantize_w([(Y, 1)], y1, "codes_y1")
-        product(Y, 0, 0, HALF, nc.scalar.copy)
+        product(Y, 0, 0, QUARTER, nc.scalar.copy)
+        product(Y, 0, QUARTER, HALF, nc.scalar.copy)
         product(Y, 0, HALF, HALF + QUARTER, nc.vector.tensor_copy)
-        product(Y, 0, HALF + QUARTER, S, nc.vector.tensor_copy)
+        product(Y, 0, HALF + QUARTER, S - P, nc.vector.tensor_copy)
+        product(Y, 0, S - P, S, nc.vector.tensor_copy)
         quantize_w([(E, 0)], e0, "codes_y0")
         whole_product(Y, 1)
         whole_product(E, 0)

@@ -52,17 +52,14 @@ def tile_picked_gatedg_none_e_kernel(tc, xT, w1, w2, w3, offs, cen, pos1, pos2, 
         cen_t = lists.tile([P, V // STRIPE], U16, name="cen_t")
         pos_t = [lists.tile([P, V // STRIPE], U16, name=f"pos_t{d}") for d in range(NEIGHBOURS)]
         planes = [keep.tile([P, T], F32, name=f"plane{j}") for j in range(PACK)]
-        w1_raw = [keep.tile([P, PACK, P], F32, name=f"w1_raw{b}") for b in range(BANDS)]
-        w2_raw = [keep.tile([P, PACK, P], F32, name=f"w2_raw{b}") for b in range(BANDS)]
-        w3_raw = keep.tile([P, PACK, N], F32, name="w3_raw")
-        w_raw = {(Y, b): w1_raw[b][:] for b in range(BANDS)}
-        for b in range(BANDS):
-            w_raw[E, b] = w2_raw[b][:]
-            w_raw[H, b] = w3_raw[:, :, b * P:(b + 1) * P]
+        w_raw = {key: keep.tile([P, PACK, P], F32, name=f"w_raw{key[0]}_{key[1]}")[:] for key in ((Y, 0), (Y, 1), (E, 0), (H, 1))}
+        late_raw = keep.tile([P, 2, PACK, P], F32, name="late_raw")
+        w_raw[E, 1], w_raw[H, 0] = late_raw[:, 0], late_raw[:, 1]
         x_rows = xT.rearrange("(p j) t -> p j t", j=PACK)
 
-        def k_rows(w):
-            return w.rearrange("(p j) n -> p j n", j=PACK)
+        def load_w(i, b):
+            rows = (w1, w2, w3)[i].rearrange("(p j) n -> p j n", j=PACK)
+            nc.sync.dma_start(out=w_raw[i, b], in_=rows[:, :, b * P:(b + 1) * P])
 
         nc.sync.dma_start(out=planes[0][:], in_=x_rows[:, 0, :])
         nc.sync.dma_start(offs_t[:], offs)
@@ -70,13 +67,14 @@ def tile_picked_gatedg_none_e_kernel(tc, xT, w1, w2, w3, offs, cen, pos1, pos2, 
             nc.sync.dma_start(out=planes[j][:], in_=x_rows[:, j, :])
         for first, last, on_vector in CHUNKS:
             nc.sync.dma_start(out=planes[LAST][:, first:last], in_=x_rows[:, LAST, first:last])
-        for b in range(BANDS):
-            nc.sync.dma_start(out=w1_raw[b][:], in_=k_rows(w1)[:, :, b * P:(b + 1) * P])
-        nc.sync.dma_start(out=w2_raw[0][:], in_=k_rows(w2)[:, :, :P])
+        load_w(Y, 0)
+        load_w(Y, 1)
+        load_w(E, 0)
+        load_w(E, 1)
         nc.sync.dma_start(cen_t[:], cen)
-        nc.sync.dma_start(out=w2_raw[1][:], in_=k_rows(w2)[:, :, P:])
-        nc.sync.dma_start(out=w3_raw[:], in_=k_rows(w3))
+        load_w(H, 0)
         nc.sync.dma_start(pos_t[0][:], pos1)
+        load_w(H, 1)
         nc.sync.dma_start(pos_t[1][:], pos2)
 
         rounded = keep.tile([P, T], BF16, name="rounded")
@@ -210,11 +208,11 @@ def tile_picked_gatedg_none_e_kernel(tc, xT, w1, w2, w3, offs, cen, pos1, pos2, 
         whole_product(Y, 1)
         whole_product(E, 0)
         late = weight_tiles([(E, 1), (H, 0)], "values_e")
-        interleave_w_on_gpsimd(E, 1)
-        interleave_w_on_gpsimd(H, 0)
+        nc.gpsimd.tensor_scalar(late[:].rearrange("p (b n) j -> p b n j", b=2), late_raw[:].rearrange("p b j n -> p b n j"),
+                                1.0, 0.0, MULT, ADD)
         fetch_centre(0)
         fetch_centre(1)
-        quantize_w([(E, 1), (H, 0)], late, f"result{Y}_1")
+        quantize_w([(E, 1), (H, 0)], late, "codes_late")
         h1 = weight_tiles([(H, 1)], "values_h1")
         interleave_w(H, 1, nc.scalar.copy)
         make_logit(0, 0)
@@ -222,10 +220,10 @@ def tile_picked_gatedg_none_e_kernel(tc, xT, w1, w2, w3, offs, cen, pos1, pos2, 
         make_logit(0, 1)
         whole_product(E, 1)
         make_gate(0, 0)
-        make_gate(0, 1)
         make_logit(1, 0)
         make_logit(1, 1)
         whole_product(H, 0)
+        make_gate(0, 1)
         make_gate(1, 0)
         whole_product(H, 1)
         make_gate(1, 1)

@@ -52,7 +52,7 @@ def tile_picked_gatedg_none_e_kernel(tc, xT, w1, w2, w3, offs, cen, pos1, pos2, 
         cen_t = lists.tile([P, V // STRIPE], U16, name="cen_t")
         pos_t = [lists.tile([P, V // STRIPE], U16, name=f"pos_t{d}") for d in range(NEIGHBOURS)]
         planes = [keep.tile([P, T], F32, name=f"plane{j}") for j in range(PACK)]
-        w_raw = {key: keep.tile([P, PACK, P], F32, name=f"w_raw{key[0]}_{key[1]}")[:] for key in ((Y, 0), (Y, 1), (E, 0), (H, 1))}
+        w_raw = {key: keep.tile([P, PACK, P], F32, name=f"w_raw{key[0]}_{key[1]}", tag=f"w_raw{key[0]}_{key[1]}", align_bytes=64)[:] for key in ((Y, 0), (Y, 1), (E, 0), (H, 1))}
         late_raw = keep.tile([P, 2, PACK, P], F32, name="late_raw")
         w_raw[E, 1], w_raw[H, 0] = late_raw[:, 0], late_raw[:, 1]
         x_rows = xT.rearrange("(p j) t -> p j t", j=PACK)
@@ -79,7 +79,7 @@ def tile_picked_gatedg_none_e_kernel(tc, xT, w1, w2, w3, offs, cen, pos1, pos2, 
 
         rounded = keep.tile([P, T], BF16, name="rounded")
         grouped = [keep.tile([P, HALF, PACK], BF16, name=f"grouped{u}", align_bytes=64) for u in range(S // HALF)]
-        x_codes = [keep.tile([P, HALF], U32, name=f"x_codes{u}", align_bytes=64) for u in range(S // HALF)]
+        x_codes = {0: keep.tile([P, QUARTER], U32, name="x_codes_first", align_bytes=64)}
         x_scales = keep.tile([P, S], U8, name="x_scales", align_bytes=64)
         w_grouped, w_codes, w_scales, results = {}, {}, {}, {}
         for i in (Y, E, H):
@@ -121,9 +121,13 @@ def tile_picked_gatedg_none_e_kernel(tc, xT, w1, w2, w3, offs, cen, pos1, pos2, 
         def quantize(codes, scales, values):
             nc.vector.quantize_mx(out=codes.bitcast(FP8X4), scales=scales, in_=values.rearrange("p c j -> p (c j)"))
 
+        def codes_of(first, last):
+            start = 0 if first < QUARTER else QUARTER
+            return x_codes[start][:, first - start:last - start]
+
         def quantize_x(first, last):
             u = first // HALF
-            quantize(x_codes[u][:, first - u * HALF:last - u * HALF], x_scales[:, first:last], grouped[u][:, first - u * HALF:last - u * HALF, :])
+            quantize(codes_of(first, last), x_scales[:, first:last], grouped[u][:, first - u * HALF:last - u * HALF, :])
 
         def interleave_w_on_gpsimd(i, b):
             nc.gpsimd.tensor_scalar(w_grouped[i, b], w_raw[i, b].rearrange("p j n -> p n j"), 1.0, 0.0, MULT, ADD)
@@ -134,11 +138,12 @@ def tile_picked_gatedg_none_e_kernel(tc, xT, w1, w2, w3, offs, cen, pos1, pos2, 
 
         def product(i, b, first, last, copy_out):
             acc = psum.tile([P, BANK], F32, name="acc")
-            u = first // HALF
-            nc.tensor.matmul_mx(out=acc[:, :last - first],
-                                lhsT=w_codes[i, b].bitcast(FP8X4), lhsT_scale=w_scales[i, b],
-                                rhs=x_codes[u][:, first - u * HALF:last - u * HALF].bitcast(FP8X4), rhs_scale=x_scales[:, first:last],
-                                start=True, stop=True)
+            borders = [first, QUARTER, last] if first < QUARTER < last else [first, last]
+            for low, high in zip(borders, borders[1:]):
+                nc.tensor.matmul_mx(out=acc[:, low - first:high - first],
+                                    lhsT=w_codes[i, b].bitcast(FP8X4), lhsT_scale=w_scales[i, b],
+                                    rhs=codes_of(low, high).bitcast(FP8X4), rhs_scale=x_scales[:, low:high],
+                                    start=True, stop=True)
             copy_out(results[i, b][:, first:last], acc[:, :last - first])
 
         def whole_product(i, b):
@@ -191,8 +196,10 @@ def tile_picked_gatedg_none_e_kernel(tc, xT, w1, w2, w3, offs, cen, pos1, pos2, 
         y1 = weight_tiles([(Y, 1)], "values_y1")
         e0 = weight_tiles([(E, 0)], "values_e")
         interleave_w_on_gpsimd(Y, 0)
-        quantize_x(0, HALF)
+        quantize_x(0, QUARTER)
         quantize_w([(Y, 0)], y0, "codes_y0")
+        x_codes[QUARTER] = keep.tile([P, S - QUARTER], U32, name="x_codes_rest", tag=f"w_raw{Y}_0", align_bytes=64)
+        quantize_x(QUARTER, HALF)
         quantize_x(HALF, HALF + QUARTER)
         quantize_x(HALF + QUARTER, S - P)
         quantize_x(S - P, S)

@@ -30,7 +30,10 @@ BANDS = N // P
 NEIGHBOURS = 2
 Y, E, H = 0, 1, 2
 RUN = 4
-CHUNKS = ((0, 2048, False), (2048, 3328, True), (3328, 3840, True), (3840, T, False))
+CHUNKS = ((0, 2048), (2048, 3328), (3328, 3840), (3840, T))
+GPSIMD_ROUNDS = ((1152, 2048),)
+SCALAR_ROUNDS = ((0, 1152), (2048, 2560), (3840, T))
+VECTOR_ROUNDS = ((2560, 3328), (3328, 3840))
 
 
 def tile_picked_gatedg_none_e_kernel(tc, xT, w1, w2, w3, offs, cen, pos1, pos2, out):
@@ -65,7 +68,7 @@ def tile_picked_gatedg_none_e_kernel(tc, xT, w1, w2, w3, offs, cen, pos1, pos2, 
         nc.sync.dma_start(offs_t[:], offs)
         for j in range(1, LAST):
             nc.sync.dma_start(out=planes[j][:], in_=x_rows[:, j, :])
-        for first, last, on_vector in CHUNKS:
+        for first, last in CHUNKS:
             nc.sync.dma_start(out=planes[LAST][:, first:last], in_=x_rows[:, LAST, first:last])
         load_w(Y, 0)
         load_w(Y, 1)
@@ -186,9 +189,12 @@ def tile_picked_gatedg_none_e_kernel(tc, xT, w1, w2, w3, offs, cen, pos1, pos2, 
         for j in range(LAST):
             for u in range(S // HALF):
                 gather_x(j, u)
-        for first, last, on_vector in CHUNKS:
-            round_chunk = nc.vector.tensor_copy if on_vector else nc.scalar.copy
-            round_chunk(rounded[:, first:last], planes[LAST][:, first:last])
+        for first, last in GPSIMD_ROUNDS:
+            nc.gpsimd.tensor_scalar(rounded[:, first:last], planes[LAST][:, first:last], 1.0, 0.0, MULT, ADD)
+        for first, last in SCALAR_ROUNDS:
+            nc.scalar.copy(rounded[:, first:last], planes[LAST][:, first:last])
+        for first, last in VECTOR_ROUNDS:
+            nc.vector.tensor_copy(rounded[:, first:last], planes[LAST][:, first:last])
         gather_x(LAST, 0)
         nc.scalar.activation(grouped[1][:, :, LAST], rounded[:].indirect(entries(offs_t, HALF, S)), COPY)
 

@@ -25,15 +25,17 @@ BANK = 512
 BANKS = 8
 HALF = S // 2
 QUARTER = S // 4
+EIGHTH = S // 8
 MID = V // 2
 BANDS = N // P
 NEIGHBOURS = 2
 Y, E, H = 0, 1, 2
 RUN = 4
+
 CHUNKS = ((0, 2048), (2048, 3328), (3328, 3840), (3840, T))
-GPSIMD_ROUNDS = ((1152, 2048),)
-SCALAR_ROUNDS = ((0, 1152), (2048, 2560), (3840, T))
-VECTOR_ROUNDS = ((2560, 3328), (3328, 3840))
+GPSIMD_ROUNDS = (1152, 2048)
+SCALAR_ROUNDS = ((0, 1152), (2048, 2560), (3328, 3584), (3840, T))
+VECTOR_ROUNDS = ((2560, 3328), (3584, 3840))
 
 
 def tile_picked_gatedg_none_e_kernel(tc, xT, w1, w2, w3, offs, cen, pos1, pos2, out):
@@ -55,9 +57,12 @@ def tile_picked_gatedg_none_e_kernel(tc, xT, w1, w2, w3, offs, cen, pos1, pos2, 
         cen_t = lists.tile([P, V // STRIPE], U16, name="cen_t")
         pos_t = [lists.tile([P, V // STRIPE], U16, name=f"pos_t{d}") for d in range(NEIGHBOURS)]
         planes = [keep.tile([P, T], F32, name=f"plane{j}") for j in range(PACK)]
-        w_raw = {key: keep.tile([P, PACK, P], F32, name=f"w_raw{key[0]}_{key[1]}", tag=f"w_raw{key[0]}_{key[1]}", align_bytes=64)[:] for key in ((Y, 0), (Y, 1), (E, 0), (H, 1))}
-        late_raw = keep.tile([P, 2, PACK, P], F32, name="late_raw")
-        w_raw[E, 1], w_raw[H, 0] = late_raw[:, 0], late_raw[:, 1]
+        pair = [(E, 1), (H, 0)]
+        w_raw = {(i, b): keep.tile([P, PACK, P], F32, name=f"w_raw{i}_{b}", tag=f"w_raw{i}_{b}", align_bytes=64)[:]
+                 for i, b in ((Y, 0), (Y, 1), (E, 0), (H, 1))}
+        pair_raw = keep.tile([P, len(pair), PACK, P], F32, name="pair_raw")
+        for n, band in enumerate(pair):
+            w_raw[band] = pair_raw[:, n]
         x_rows = xT.rearrange("(p j) t -> p j t", j=PACK)
 
         def load_w(i, b):
@@ -70,10 +75,9 @@ def tile_picked_gatedg_none_e_kernel(tc, xT, w1, w2, w3, offs, cen, pos1, pos2, 
             nc.sync.dma_start(out=planes[j][:], in_=x_rows[:, j, :])
         for first, last in CHUNKS:
             nc.sync.dma_start(out=planes[LAST][:, first:last], in_=x_rows[:, LAST, first:last])
-        load_w(Y, 0)
-        load_w(Y, 1)
-        load_w(E, 0)
-        load_w(E, 1)
+        for i in (Y, E):
+            for b in range(BANDS):
+                load_w(i, b)
         nc.sync.dma_start(cen_t[:], cen)
         load_w(H, 0)
         nc.sync.dma_start(pos_t[0][:], pos1)
@@ -84,29 +88,8 @@ def tile_picked_gatedg_none_e_kernel(tc, xT, w1, w2, w3, offs, cen, pos1, pos2, 
         grouped = [keep.tile([P, HALF, PACK], BF16, name=f"grouped{u}", align_bytes=64) for u in range(S // HALF)]
         x_codes = {0: keep.tile([P, QUARTER], U32, name="x_codes_first", align_bytes=64)}
         x_scales = keep.tile([P, S], U8, name="x_scales", align_bytes=64)
-        w_grouped, w_codes, w_scales, results = {}, {}, {}, {}
-        for i in (Y, E, H):
-            for b in range(BANDS):
-                results[i, b] = keep.tile([P, S], F32, name=f"result{i}_{b}", tag=f"result{i}_{b}", align_bytes=64)
-
-        def weight_tiles(keys, grouped_tag):
-            width = len(keys) * P
-            name = f"{keys[0][0]}_{keys[0][1]}"
-            values = keep.tile([P, width, PACK], BF16, name=f"w_grouped{name}", tag=grouped_tag, align_bytes=64)
-            for n, key in enumerate(keys):
-                w_grouped[key] = values[:, n * P:(n + 1) * P, :]
-            return values
-
-        def quantize_w(keys, values, codes_tag):
-            width = len(keys) * P
-            name = f"{keys[0][0]}_{keys[0][1]}"
-            codes = keep.tile([P, width], U32, name=f"w_codes{name}", tag=codes_tag, align_bytes=64)
-            scales = keep.tile([P, width], U8, name=f"w_scales{name}", align_bytes=64)
-            for n, key in enumerate(keys):
-                w_codes[key] = codes[:, n * P:(n + 1) * P]
-                w_scales[key] = scales[:, n * P:(n + 1) * P]
-            quantize(codes[:], scales[:], values[:])
-
+        w_grouped, w_codes, w_scales = {}, {}, {}
+        results = {(i, b): keep.tile([P, S], F32, name=f"result{i}_{b}", align_bytes=64) for i in (Y, E, H) for b in range(BANDS)}
         centre = [keep.tile([P, V], F32, name=f"centre{b}") for b in range(BANDS)]
         total = [keep.tile([P, V], F32, name=f"total{b}") for b in range(BANDS)]
         edges = [(b, d) for b in range(BANDS) for d in range(NEIGHBOURS)]
@@ -132,12 +115,28 @@ def tile_picked_gatedg_none_e_kernel(tc, xT, w1, w2, w3, offs, cen, pos1, pos2, 
             u = first // HALF
             quantize(codes_of(first, last), x_scales[:, first:last], grouped[u][:, first - u * HALF:last - u * HALF, :])
 
-        def interleave_w_on_gpsimd(i, b):
-            nc.gpsimd.tensor_scalar(w_grouped[i, b], w_raw[i, b].rearrange("p j n -> p n j"), 1.0, 0.0, MULT, ADD)
+        def grouped_tile(bands, slot):
+            values = keep.tile([P, len(bands) * P, PACK], BF16, name=f"w_grouped{bands[0][0]}_{bands[0][1]}", tag=slot,
+                               align_bytes=64)
+            for n, band in enumerate(bands):
+                w_grouped[band] = values[:, n * P:(n + 1) * P, :]
+            return values
 
-        def interleave_w(i, b, copy):
-            copy(w_grouped[i, b].rearrange("p (c n) j -> p c j n", n=RUN),
-                 w_raw[i, b].rearrange("p j (c n) -> p c j n", n=RUN))
+        def quantize_w(bands, values, slot):
+            name = f"{bands[0][0]}_{bands[0][1]}"
+            codes = keep.tile([P, len(bands) * P], U32, name=f"w_codes{name}", tag=slot, align_bytes=64)
+            scales = keep.tile([P, len(bands) * P], U8, name=f"w_scales{name}", align_bytes=64)
+            for n, band in enumerate(bands):
+                w_codes[band] = codes[:, n * P:(n + 1) * P]
+                w_scales[band] = scales[:, n * P:(n + 1) * P]
+            quantize(codes[:], scales[:], values[:])
+
+        def round_on_gpsimd(dst, src):
+            nc.gpsimd.tensor_scalar(dst, src, 1.0, 0.0, MULT, ADD)
+
+        def interleave_on_scalar(i, b):
+            nc.scalar.copy(w_grouped[i, b].rearrange("p (c n) j -> p c j n", n=RUN),
+                           w_raw[i, b].rearrange("p j (c n) -> p c j n", n=RUN))
 
         def product(i, b, first, last, copy_out):
             acc = psum.tile([P, BANK], F32, name="acc")
@@ -182,15 +181,14 @@ def tile_picked_gatedg_none_e_kernel(tc, xT, w1, w2, w3, offs, cen, pos1, pos2, 
             nc.scalar.copy(total[b][:, first:last], acc[:, first:last])
             nc.scalar.dma_start(out=out[b * P:(b + 1) * P, first:last], in_=total[b][:, first:last])
 
-        def add_and_store(b, first, last):
+        def add_and_store(b, first, last, queue):
             nc.vector.tensor_tensor(total[b][:, first:last], message[b, 0][:, first:last], message[b, 1][:, first:last], ADD)
-            nc.sync.dma_start(out=out[b * P:(b + 1) * P, first:last], in_=total[b][:, first:last])
+            queue.dma_start(out=out[b * P:(b + 1) * P, first:last], in_=total[b][:, first:last])
 
         for j in range(LAST):
             for u in range(S // HALF):
                 gather_x(j, u)
-        for first, last in GPSIMD_ROUNDS:
-            nc.gpsimd.tensor_scalar(rounded[:, first:last], planes[LAST][:, first:last], 1.0, 0.0, MULT, ADD)
+        round_on_gpsimd(rounded[:, slice(*GPSIMD_ROUNDS)], planes[LAST][:, slice(*GPSIMD_ROUNDS)])
         for first, last in SCALAR_ROUNDS:
             nc.scalar.copy(rounded[:, first:last], planes[LAST][:, first:last])
         for first, last in VECTOR_ROUNDS:
@@ -198,48 +196,50 @@ def tile_picked_gatedg_none_e_kernel(tc, xT, w1, w2, w3, offs, cen, pos1, pos2, 
         gather_x(LAST, 0)
         nc.scalar.activation(grouped[1][:, :, LAST], rounded[:].indirect(entries(offs_t, HALF, S)), COPY)
 
-        y0 = weight_tiles([(Y, 0)], "values_y0")
-        y1 = weight_tiles([(Y, 1)], "values_y1")
-        e0 = weight_tiles([(E, 0)], "values_e")
-        interleave_w_on_gpsimd(Y, 0)
+        y0 = grouped_tile([(Y, 0)], "values_y0")
+        y1 = grouped_tile([(Y, 1)], "values_y1")
+        e0 = grouped_tile([(E, 0)], "values_e")
+        round_on_gpsimd(w_grouped[Y, 0], w_raw[Y, 0].rearrange("p j n -> p n j"))
         quantize_x(0, QUARTER)
         quantize_w([(Y, 0)], y0, "codes_y0")
         x_codes[QUARTER] = keep.tile([P, S - QUARTER], U32, name="x_codes_rest", tag=f"w_raw{Y}_0", align_bytes=64)
         quantize_x(QUARTER, HALF)
         quantize_x(HALF, HALF + QUARTER)
-        quantize_x(HALF + QUARTER, S - P)
-        quantize_x(S - P, S)
-        interleave_w(Y, 1, nc.scalar.copy)
-        interleave_w(E, 0, nc.scalar.copy)
+        quantize_x(HALF + QUARTER, S - EIGHTH)
+        quantize_x(S - EIGHTH, S)
+        interleave_on_scalar(Y, 1)
+        interleave_on_scalar(E, 0)
         quantize_w([(Y, 1)], y1, "codes_y1")
         product(Y, 0, 0, QUARTER, nc.scalar.copy)
         product(Y, 0, QUARTER, HALF, nc.scalar.copy)
         product(Y, 0, HALF, HALF + QUARTER, nc.vector.tensor_copy)
-        product(Y, 0, HALF + QUARTER, S - P, nc.vector.tensor_copy)
-        product(Y, 0, S - P, S, nc.vector.tensor_copy)
+        product(Y, 0, HALF + QUARTER, S - EIGHTH, nc.vector.tensor_copy)
+        product(Y, 0, S - EIGHTH, S, nc.vector.tensor_copy)
         quantize_w([(E, 0)], e0, "codes_y0")
         whole_product(Y, 1)
         whole_product(E, 0)
-        late = weight_tiles([(E, 1), (H, 0)], "values_e")
-        nc.gpsimd.tensor_scalar(late[:].rearrange("p (b n) j -> p b n j", b=2), late_raw[:].rearrange("p b j n -> p b n j"),
-                                1.0, 0.0, MULT, ADD)
-        fetch_centre(0)
-        fetch_centre(1)
-        quantize_w([(E, 1), (H, 0)], late, "codes_late")
-        h1 = weight_tiles([(H, 1)], "values_h1")
-        interleave_w(H, 1, nc.scalar.copy)
+
+        pair_values = grouped_tile(pair, "values_e")
+        round_on_gpsimd(pair_values[:].rearrange("p (b n) j -> p b n j", b=len(pair)), pair_raw[:].rearrange("p b j n -> p b n j"))
+        for b in range(BANDS):
+            fetch_centre(b)
+        quantize_w(pair, pair_values, "codes_pair")
+        h1 = grouped_tile([(H, 1)], "values_h1")
+        interleave_on_scalar(H, 1)
         make_logit(0, 0)
         quantize_w([(H, 1)], h1, "codes_h1")
         make_logit(0, 1)
-        whole_product(E, 1)
+        for first, last in ((0, QUARTER), (QUARTER, HALF), (HALF, S)):
+            product(E, 1, first, last, nc.scalar.copy)
         make_gate(0, 0)
-        make_logit(1, 0)
-        make_logit(1, 1)
+        for d in range(NEIGHBOURS):
+            make_logit(1, d)
         whole_product(H, 0)
         make_gate(0, 1)
         make_gate(1, 0)
         whole_product(H, 1)
         make_gate(1, 1)
+
         make_message(0, 0, 0, V)
         for first in (0, MID):
             make_message(0, 1, first, first + MID)
@@ -250,5 +250,5 @@ def tile_picked_gatedg_none_e_kernel(tc, xT, w1, w2, w3, offs, cen, pos1, pos2, 
         make_message(1, 0, 0, V)
         for first in (0, MID):
             make_message(1, 1, first, first + MID)
-        for first in (0, MID):
-            add_and_store(1, first, first + MID)
+        add_and_store(1, 0, MID, nc.sync)
+        add_and_store(1, MID, V, nc.scalar)

@@ -138,7 +138,7 @@ def tile_picked_gatedg_none_e_kernel(tc, xT, w1, w2, w3, offs, cen, pos1, pos2, 
             nc.scalar.copy(w_grouped[i, b].rearrange("p (c n) j -> p c j n", n=RUN),
                            w_raw[i, b].rearrange("p j (c n) -> p c j n", n=RUN))
 
-        def product(i, b, first, last, copy_out):
+        def multiply(i, b, first, last):
             acc = psum.tile([P, BANK], F32, name="acc")
             borders = [first, QUARTER, last] if first < QUARTER < last else [first, last]
             for low, high in zip(borders, borders[1:]):
@@ -146,14 +146,17 @@ def tile_picked_gatedg_none_e_kernel(tc, xT, w1, w2, w3, offs, cen, pos1, pos2, 
                                     lhsT=w_codes[i, b].bitcast(FP8X4), lhsT_scale=w_scales[i, b],
                                     rhs=codes_of(low, high).bitcast(FP8X4), rhs_scale=x_scales[:, low:high],
                                     start=True, stop=True)
-            copy_out(results[i, b][:, first:last], acc[:, :last - first])
+            return acc
+
+        def product(i, b, first, last, copy_out):
+            copy_out(results[i, b][:, first:last], multiply(i, b, first, last)[:, :last - first])
 
         def whole_product(i, b):
             for first in range(0, S, BANK):
                 product(i, b, first, first + BANK, nc.scalar.copy)
 
-        def fetch_centre(b):
-            nc.vector.tensor_copy(centre[b][:], results[Y, b][:].indirect(cen_t[:]))
+        def centre_source(b, first, last):
+            return results[Y, b][:].indirect(entries(cen_t, first, last))
 
         def make_logit(b, d):
             nc.vector.tensor_tensor(logit[b, d][:], results[E, b][:].indirect(pos_t[d][:]), centre[b][:], ADD)
@@ -221,20 +224,23 @@ def tile_picked_gatedg_none_e_kernel(tc, xT, w1, w2, w3, offs, cen, pos1, pos2, 
 
         pair_values = grouped_tile(pair, "values_e")
         round_on_gpsimd(pair_values[:].rearrange("p (b n) j -> p b n j", b=len(pair)), pair_raw[:].rearrange("p b j n -> p b n j"))
-        for b in range(BANDS):
-            fetch_centre(b)
+        nc.vector.tensor_copy(centre[0][:], centre_source(0, 0, V))
+        nc.vector.tensor_copy(centre[1][:, :MID], centre_source(1, 0, MID))
+        nc.scalar.activation(centre[1][:, MID:], centre_source(1, MID, V), COPY)
         quantize_w(pair, pair_values, "codes_pair")
-        h1 = grouped_tile([(H, 1)], "values_h1")
-        interleave_on_scalar(H, 1)
         make_logit(0, 0)
-        quantize_w([(H, 1)], h1, "codes_h1")
         make_logit(0, 1)
         for first, last in ((0, QUARTER), (QUARTER, HALF), (HALF, S)):
             product(E, 1, first, last, nc.scalar.copy)
         make_gate(0, 0)
-        for d in range(NEIGHBOURS):
-            make_logit(1, d)
-        whole_product(H, 0)
+        h0_banks = [multiply(H, 0, first, first + BANK) for first in range(0, S, BANK)]
+        h1 = grouped_tile([(H, 1)], "codes_pair")
+        interleave_on_scalar(H, 1)
+        make_logit(1, 0)
+        quantize_w([(H, 1)], h1, "codes_h1")
+        make_logit(1, 1)
+        for n, acc in enumerate(h0_banks):
+            nc.scalar.copy(results[H, 0][:, n * BANK:(n + 1) * BANK], acc[:])
         make_gate(0, 1)
         make_gate(1, 0)
         whole_product(H, 1)

@@ -27,6 +27,7 @@ HALF = S // 2
 QUARTER = S // 4
 EIGHTH = S // 8
 MID = V // 2
+SHARE = 3 * V // 4
 BANDS = N // P
 NEIGHBOURS = 2
 Y, E, H = 0, 1, 2
@@ -96,6 +97,7 @@ def tile_picked_gatedg_none_e_kernel(tc, xT, w1, w2, w3, offs, cen, pos1, pos2, 
         message = {(b, d): keep.tile([P, V], F32, name=f"message{b}_{d}") for b, d in edges}
         logit = {(b, d): keep.tile([P, V], F32, name=f"logit{b}_{d}") for b, d in edges}
         gate = {(b, d): keep.tile([P, V], F32, name=f"gate{b}_{d}") for b, d in edges}
+        fetched = keep.tile([P, V], F32, name="fetched")
         turned = keep.tile([P, V], F32, name="turned")
 
         def entries(list_tile, first, last):
@@ -225,26 +227,25 @@ def tile_picked_gatedg_none_e_kernel(tc, xT, w1, w2, w3, offs, cen, pos1, pos2, 
         pair_values = grouped_tile(pair, "values_e")
         round_on_gpsimd(pair_values[:].rearrange("p (b n) j -> p b n j", b=len(pair)), pair_raw[:].rearrange("p b j n -> p b n j"))
         nc.vector.tensor_copy(centre[0][:], centre_source(0, 0, V))
-        nc.vector.tensor_copy(centre[1][:, :MID], centre_source(1, 0, MID))
-        nc.scalar.activation(centre[1][:, MID:], centre_source(1, MID, V), COPY)
+        nc.vector.tensor_copy(centre[1][:, :SHARE], centre_source(1, 0, SHARE))
+        nc.scalar.activation(centre[1][:, SHARE:], centre_source(1, SHARE, V), COPY)
         quantize_w(pair, pair_values, "codes_pair")
+        h1 = grouped_tile([(H, 1)], "values_h1")
+        interleave_on_scalar(H, 1)
         make_logit(0, 0)
+        quantize_w([(H, 1)], h1, "codes_h1")
         make_logit(0, 1)
         for first, last in ((0, QUARTER), (QUARTER, HALF), (HALF, S)):
             product(E, 1, first, last, nc.scalar.copy)
         make_gate(0, 0)
-        h0_banks = [multiply(H, 0, first, first + BANK) for first in range(0, S, BANK)]
-        h1 = grouped_tile([(H, 1)], "codes_pair")
-        interleave_on_scalar(H, 1)
-        make_logit(1, 0)
-        quantize_w([(H, 1)], h1, "codes_h1")
-        make_logit(1, 1)
-        for n, acc in enumerate(h0_banks):
-            nc.scalar.copy(results[H, 0][:, n * BANK:(n + 1) * BANK], acc[:])
+        for d in range(NEIGHBOURS):
+            make_logit(1, d)
+        whole_product(H, 0)
         make_gate(0, 1)
         make_gate(1, 0)
         whole_product(H, 1)
         make_gate(1, 1)
+        nc.scalar.activation(fetched[:, MID:], results[H, 1][:].indirect(entries(pos_t[1], MID, V)), COPY)
 
         make_message(0, 0, 0, V)
         for first in (0, MID):
@@ -254,7 +255,7 @@ def tile_picked_gatedg_none_e_kernel(tc, xT, w1, w2, w3, offs, cen, pos1, pos2, 
         for first in (0, MID):
             turn_back_and_store(0, first, first + MID)
         make_message(1, 0, 0, V)
-        for first in (0, MID):
-            make_message(1, 1, first, first + MID)
+        make_message(1, 1, 0, MID)
+        nc.vector.tensor_tensor(message[1, 1][:, MID:], fetched[:, MID:], gate[1, 1][:, MID:], MULT)
         add_and_store(1, 0, MID, nc.sync)
         add_and_store(1, MID, V, nc.scalar)

@@ -95,7 +95,7 @@ def tile_picked_gatedg_none_e_kernel(tc, xT, w1, w2, w3, offs, cen, pos1, pos2, 
         total = [keep.tile([P, V], F32, name=f"total{b}") for b in range(BANDS)]
         edges = [(b, d) for b in range(BANDS) for d in range(NEIGHBOURS)]
         message = {(b, d): keep.tile([P, V], F32, name=f"message{b}_{d}") for b, d in edges}
-        logit = {(b, d): keep.tile([P, V], F32, name=f"logit{b}_{d}") for b, d in edges}
+        logit = {(b, d): keep.tile([P, V], F32, name=f"logit{b}_{d}", tag=f"logit{b}_{d}") for b, d in edges[:-1]}
         gate = {(b, d): keep.tile([P, V], F32, name=f"gate{b}_{d}") for b, d in edges}
         fetched = keep.tile([P, V], F32, name="fetched")
         turned = keep.tile([P, V], F32, name="turned")
@@ -238,24 +238,26 @@ def tile_picked_gatedg_none_e_kernel(tc, xT, w1, w2, w3, offs, cen, pos1, pos2, 
         for first, last in ((0, QUARTER), (QUARTER, HALF), (HALF, S)):
             product(E, 1, first, last, nc.scalar.copy)
         make_gate(0, 0)
-        for d in range(NEIGHBOURS):
-            make_logit(1, d)
+        make_logit(1, 0)
         whole_product(H, 0)
         make_gate(0, 1)
-        make_gate(1, 0)
-        whole_product(H, 1)
-        make_gate(1, 1)
-        nc.scalar.activation(fetched[:, MID:], results[H, 1][:].indirect(entries(pos_t[1], MID, V)), COPY)
 
         make_message(0, 0, 0, V)
         for first in (0, MID):
             make_message(0, 1, first, first + MID)
+        logit[1, 1] = keep.tile([P, V], F32, name="logit1_1", tag="logit0_1")
+        make_logit(1, 1)
+        whole_product(H, 1)
+        make_gate(1, 0)
+        nc.scalar.activation(fetched[:], results[H, 1][:].indirect(pos_t[1][:]), COPY)
         for first in (0, MID):
             add_turned(0, first, first + MID)
+        make_gate(1, 1)
         for first in (0, MID):
             turn_back_and_store(0, first, first + MID)
         make_message(1, 0, 0, V)
-        make_message(1, 1, 0, MID)
-        nc.vector.tensor_tensor(message[1, 1][:, MID:], fetched[:, MID:], gate[1, 1][:, MID:], MULT)
+        for first in (0, MID):
+            cols = slice(first, first + MID)
+            nc.vector.tensor_tensor(message[1, 1][:, cols], fetched[:, cols], gate[1, 1][:, cols], MULT)
         add_and_store(1, 0, MID, nc.sync)
         add_and_store(1, MID, V, nc.scalar)

@@ -33,10 +33,10 @@ NEIGHBOURS = 2
 Y, E, H = 0, 1, 2
 RUN = 4
 
-CHUNKS = ((0, 2048), (2048, 3328), (3328, 3840), (3840, T))
+CHUNKS = ((0, 2048), (2048, 3456), (3456, 3968), (3968, T))
 GPSIMD_ROUNDS = (1152, 2048)
-SCALAR_ROUNDS = ((0, 1152), (2048, 2560), (3328, 3584), (3840, T))
-VECTOR_ROUNDS = ((2560, 3328), (3584, 3840))
+SCALAR_ROUNDS = ((0, 1152), (2048, 2560), (3456, 3584), (3968, T))
+VECTOR_ROUNDS = ((2560, 3456), (3584, 3968))
 
 
 def tile_picked_gatedg_none_e_kernel(tc, xT, w1, w2, w3, offs, cen, pos1, pos2, out):
@@ -44,6 +44,7 @@ def tile_picked_gatedg_none_e_kernel(tc, xT, w1, w2, w3, offs, cen, pos1, pos2, 
     with ExitStack() as ctx:
         lists = ctx.enter_context(tc.tile_pool(name="lists", bufs=1))
         keep = ctx.enter_context(tc.tile_pool(name="keep", bufs=1))
+        shared = ctx.enter_context(tc.tile_pool(name="shared", bufs=1))
         psum = ctx.enter_context(tc.psum_pool(name="psum", bufs=BANKS))
 
         warm_in = keep.tile([P, 1], F32, name="warm_in")
@@ -60,7 +61,8 @@ def tile_picked_gatedg_none_e_kernel(tc, xT, w1, w2, w3, offs, cen, pos1, pos2, 
         planes = [keep.tile([P, T], F32, name=f"plane{j}") for j in range(PACK)]
         pair = [(E, 1), (H, 0)]
         w_raw = {(i, b): keep.tile([P, PACK, P], F32, name=f"w_raw{i}_{b}", tag=f"w_raw{i}_{b}", align_bytes=64)[:]
-                 for i, b in ((Y, 0), (Y, 1), (E, 0), (H, 1))}
+                 for i, b in ((Y, 1), (E, 0), (H, 1))}
+        w_raw[Y, 0] = shared.tile([P, PACK, P], F32, name="w_raw0_0", align_bytes=64, offset=0)[:]
         pair_raw = keep.tile([P, len(pair), PACK, P], F32, name="pair_raw")
         for n, band in enumerate(pair):
             w_raw[band] = pair_raw[:, n]
@@ -87,7 +89,7 @@ def tile_picked_gatedg_none_e_kernel(tc, xT, w1, w2, w3, offs, cen, pos1, pos2, 
 
         rounded = keep.tile([P, T], BF16, name="rounded")
         grouped = [keep.tile([P, HALF, PACK], BF16, name=f"grouped{u}", align_bytes=64) for u in range(S // HALF)]
-        x_codes = {0: keep.tile([P, QUARTER], U32, name="x_codes_first", align_bytes=64)}
+        x_codes = {}
         x_scales = keep.tile([P, S], U8, name="x_scales", align_bytes=64)
         w_grouped, w_codes, w_scales = {}, {}, {}
         results = {(i, b): keep.tile([P, S], F32, name=f"result{i}_{b}", align_bytes=64) for i in (Y, E, H) for b in range(BANDS)}
@@ -205,9 +207,10 @@ def tile_picked_gatedg_none_e_kernel(tc, xT, w1, w2, w3, offs, cen, pos1, pos2, 
         y1 = grouped_tile([(Y, 1)], "values_y1")
         e0 = grouped_tile([(E, 0)], "values_e")
         round_on_gpsimd(w_grouped[Y, 0], w_raw[Y, 0].rearrange("p j n -> p n j"))
-        quantize_x(0, QUARTER)
         quantize_w([(Y, 0)], y0, "codes_y0")
-        x_codes[QUARTER] = keep.tile([P, S - QUARTER], U32, name="x_codes_rest", tag=f"w_raw{Y}_0", align_bytes=64)
+        x_codes[0] = shared.tile([P, QUARTER], U32, name="x_codes_first", align_bytes=64, offset=0)
+        quantize_x(0, QUARTER)
+        x_codes[QUARTER] = shared.tile([P, S - QUARTER], U32, name="x_codes_rest", align_bytes=64, offset=4 * QUARTER)
         quantize_x(QUARTER, HALF)
         quantize_x(HALF, HALF + QUARTER)
         quantize_x(HALF + QUARTER, S - EIGHTH)
@@ -218,7 +221,7 @@ def tile_picked_gatedg_none_e_kernel(tc, xT, w1, w2, w3, offs, cen, pos1, pos2, 
         product(Y, 0, 0, QUARTER, nc.scalar.copy)
         product(Y, 0, QUARTER, HALF, nc.scalar.copy)
         product(Y, 0, HALF, HALF + QUARTER, nc.vector.tensor_copy)
-        product(Y, 0, HALF + QUARTER, S - EIGHTH, nc.vector.tensor_copy)
+        product(Y, 0, HALF + QUARTER, S - EIGHTH, nc.scalar.copy)
         product(Y, 0, S - EIGHTH, S, nc.vector.tensor_copy)
         quantize_w([(E, 0)], e0, "codes_y0")
         whole_product(Y, 1)

@@ -186,7 +186,7 @@ def tile_picked_gatedg_none_e_kernel(tc, xT, w1, w2, w3, offs, cen, pos1, pos2, 
             for c in range(first, last, P):
                 nc.tensor.transpose(acc[:, c:c + P], turned[:, c:c + P], identity[:])
             nc.scalar.copy(total[b][:, first:last], acc[:, first:last])
-            nc.scalar.dma_start(out=out[b * P:(b + 1) * P, first:last], in_=total[b][:, first:last])
+            nc.sync.dma_start(out=out[b * P:(b + 1) * P, first:last], in_=total[b][:, first:last])
 
         def add_and_store(b, first, last, queue):
             nc.vector.tensor_tensor(total[b][:, first:last], message[b, 0][:, first:last], message[b, 1][:, first:last], ADD)
@@ -263,4 +263,4 @@ def tile_picked_gatedg_none_e_kernel(tc, xT, w1, w2, w3, offs, cen, pos1, pos2, 
             cols = slice(first, first + MID)
             nc.vector.tensor_tensor(message[1, 1][:, cols], fetched[:, cols], gate[1, 1][:, cols], MULT)
         add_and_store(1, 0, MID, nc.sync)
-        add_and_store(1, MID, V, nc.scalar)
+        add_and_store(1, MID, V, nc.sync)

@@ -44,7 +44,6 @@ def tile_picked_gatedg_none_e_kernel(tc, xT, w1, w2, w3, offs, cen, pos1, pos2, 
     with ExitStack() as ctx:
         lists = ctx.enter_context(tc.tile_pool(name="lists", bufs=1))
         keep = ctx.enter_context(tc.tile_pool(name="keep", bufs=1))
-        shared = ctx.enter_context(tc.tile_pool(name="shared", bufs=1))
         psum = ctx.enter_context(tc.psum_pool(name="psum", bufs=BANKS))
 
         warm_in = keep.tile([P, 1], F32, name="warm_in")
@@ -61,8 +60,7 @@ def tile_picked_gatedg_none_e_kernel(tc, xT, w1, w2, w3, offs, cen, pos1, pos2, 
         planes = [keep.tile([P, T], F32, name=f"plane{j}") for j in range(PACK)]
         pair = [(E, 1), (H, 0)]
         w_raw = {(i, b): keep.tile([P, PACK, P], F32, name=f"w_raw{i}_{b}", tag=f"w_raw{i}_{b}", align_bytes=64)[:]
-                 for i, b in ((Y, 1), (E, 0), (H, 1))}
-        w_raw[Y, 0] = shared.tile([P, PACK, P], F32, name="w_raw0_0", align_bytes=64, offset=0)[:]
+                 for i, b in ((Y, 0), (Y, 1), (E, 0), (H, 1))}
         pair_raw = keep.tile([P, len(pair), PACK, P], F32, name="pair_raw")
         for n, band in enumerate(pair):
             w_raw[band] = pair_raw[:, n]
@@ -89,7 +87,6 @@ def tile_picked_gatedg_none_e_kernel(tc, xT, w1, w2, w3, offs, cen, pos1, pos2, 
 
         rounded = keep.tile([P, T], BF16, name="rounded")
         grouped = [keep.tile([P, HALF, PACK], BF16, name=f"grouped{u}", align_bytes=64) for u in range(S // HALF)]
-        x_codes = {}
         x_scales = keep.tile([P, S], U8, name="x_scales", align_bytes=64)
         w_grouped, w_codes, w_scales = {}, {}, {}
         results = {(i, b): keep.tile([P, S], F32, name=f"result{i}_{b}", align_bytes=64) for i in (Y, E, H) for b in range(BANDS)}
@@ -111,13 +108,9 @@ def tile_picked_gatedg_none_e_kernel(tc, xT, w1, w2, w3, offs, cen, pos1, pos2, 
         def quantize(codes, scales, values):
             nc.vector.quantize_mx(out=codes.bitcast(FP8X4), scales=scales, in_=values.rearrange("p c j -> p (c j)"))
 
-        def codes_of(first, last):
-            start = 0 if first < QUARTER else QUARTER
-            return x_codes[start][:, first - start:last - start]
-
         def quantize_x(first, last):
             u = first // HALF
-            quantize(codes_of(first, last), x_scales[:, first:last], grouped[u][:, first - u * HALF:last - u * HALF, :])
+            quantize(x_codes[:, first:last], x_scales[:, first:last], grouped[u][:, first - u * HALF:last - u * HALF, :])
 
         def grouped_tile(bands, slot):
             values = keep.tile([P, len(bands) * P, PACK], BF16, name=f"w_grouped{bands[0][0]}_{bands[0][1]}", tag=slot,
@@ -144,12 +137,9 @@ def tile_picked_gatedg_none_e_kernel(tc, xT, w1, w2, w3, offs, cen, pos1, pos2, 
 
         def multiply(i, b, first, last):
             acc = psum.tile([P, BANK], F32, name="acc")
-            borders = [first, QUARTER, last] if first < QUARTER < last else [first, last]
-            for low, high in zip(borders, borders[1:]):
-                nc.tensor.matmul_mx(out=acc[:, low - first:high - first],
-                                    lhsT=w_codes[i, b].bitcast(FP8X4), lhsT_scale=w_scales[i, b],
-                                    rhs=codes_of(low, high).bitcast(FP8X4), rhs_scale=x_scales[:, low:high],
-                                    start=True, stop=True)
+            nc.tensor.matmul_mx(out=acc[:, :last - first], lhsT=w_codes[i, b].bitcast(FP8X4), lhsT_scale=w_scales[i, b],
+                                rhs=x_codes[:, first:last].bitcast(FP8X4), rhs_scale=x_scales[:, first:last],
+                                start=True, stop=True)
             return acc
 
         def product(i, b, first, last, copy_out):
@@ -188,9 +178,9 @@ def tile_picked_gatedg_none_e_kernel(tc, xT, w1, w2, w3, offs, cen, pos1, pos2, 
             nc.scalar.copy(total[b][:, first:last], acc[:, first:last])
             nc.sync.dma_start(out=out[b * P:(b + 1) * P, first:last], in_=total[b][:, first:last])
 
-        def add_and_store(b, first, last, queue):
+        def add_and_store(b, first, last):
             nc.vector.tensor_tensor(total[b][:, first:last], message[b, 0][:, first:last], message[b, 1][:, first:last], ADD)
-            queue.dma_start(out=out[b * P:(b + 1) * P, first:last], in_=total[b][:, first:last])
+            nc.sync.dma_start(out=out[b * P:(b + 1) * P, first:last], in_=total[b][:, first:last])
 
         for j in range(LAST):
             for u in range(S // HALF):
@@ -208,9 +198,8 @@ def tile_picked_gatedg_none_e_kernel(tc, xT, w1, w2, w3, offs, cen, pos1, pos2, 
         e0 = grouped_tile([(E, 0)], "values_e")
         round_on_gpsimd(w_grouped[Y, 0], w_raw[Y, 0].rearrange("p j n -> p n j"))
         quantize_w([(Y, 0)], y0, "codes_y0")
-        x_codes[0] = shared.tile([P, QUARTER], U32, name="x_codes_first", align_bytes=64, offset=0)
+        x_codes = keep.tile([P, S], U32, name="x_codes", tag=f"w_raw{Y}_0", align_bytes=64)
         quantize_x(0, QUARTER)
-        x_codes[QUARTER] = shared.tile([P, S - QUARTER], U32, name="x_codes_rest", align_bytes=64, offset=4 * QUARTER)
         quantize_x(QUARTER, HALF)
         quantize_x(HALF, HALF + QUARTER)
         quantize_x(HALF + QUARTER, S - EIGHTH)
@@ -262,5 +251,5 @@ def tile_picked_gatedg_none_e_kernel(tc, xT, w1, w2, w3, offs, cen, pos1, pos2, 
         for first in (0, MID):
             cols = slice(first, first + MID)
             nc.vector.tensor_tensor(message[1, 1][:, cols], fetched[:, cols], gate[1, 1][:, cols], MULT)
-        add_and_store(1, 0, MID, nc.sync)
-        add_and_store(1, MID, V, nc.sync)
+        for first in (0, MID):
+            add_and_store(1, first, first + MID)

from contextlib import ExitStack

import concourse.mybir as mybir
from concourse.masks import make_identity

K, T, S, V, N = 512, 4096, 1024, 512, 256
FLOPS = 3 * 2 * K * N * S

F32 = mybir.dt.float32
BF16 = mybir.dt.bfloat16
U32 = mybir.dt.uint32
U16 = mybir.dt.uint16
U8 = mybir.dt.uint8
FP8X4 = mybir.dt.float8_e4m3fn_x4
ADD = mybir.AluOpType.add
MULT = mybir.AluOpType.mult
SIGMOID = mybir.ActivationFunctionType.Sigmoid
COPY = mybir.ActivationFunctionType.Copy

P = 128
PACK = 4
LAST = PACK - 1
STRIPE = 16
BANK = 512
BANKS = 8
HALF = S // 2
QUARTER = S // 4
EIGHTH = S // 8
MID = V // 2
SHARE = 3 * V // 4
BANDS = N // P
NEIGHBOURS = 2
Y, E, H = 0, 1, 2
RUN = 4

CHUNKS = ((0, 2048), (2048, 3456), (3456, 3968), (3968, T))
GPSIMD_ROUNDS = (1152, 2048)
SCALAR_ROUNDS = ((0, 1152), (2048, 2560), (3456, 3584), (3968, T))
VECTOR_ROUNDS = ((2560, 3456), (3584, 3968))


def tile_picked_gatedg_none_e_kernel(tc, xT, w1, w2, w3, offs, cen, pos1, pos2, out):
    nc = tc.nc
    with ExitStack() as ctx:
        lists = ctx.enter_context(tc.tile_pool(name="lists", bufs=1))
        keep = ctx.enter_context(tc.tile_pool(name="keep", bufs=1))
        psum = ctx.enter_context(tc.psum_pool(name="psum", bufs=BANKS))

        warm_in = keep.tile([P, 1], F32, name="warm_in")
        warm_out = keep.tile([P, 1], F32, name="warm_out")
        nc.vector.memset(warm_in[:], 0.0)
        nc.scalar.activation(warm_out[:], warm_in[:], SIGMOID)

        identity = keep.tile([P, P], F32, name="identity")
        make_identity(nc, identity[:])

        offs_t = lists.tile([P, S // STRIPE], U16, name="offs_t")
        cen_t = lists.tile([P, V // STRIPE], U16, name="cen_t")
        pos_t = [lists.tile([P, V // STRIPE], U16, name=f"pos_t{d}") for d in range(NEIGHBOURS)]
        planes = [keep.tile([P, T], F32, name=f"plane{j}") for j in range(PACK)]
        pair = [(E, 1), (H, 0)]
        w_raw = {(i, b): keep.tile([P, PACK, P], F32, name=f"w_raw{i}_{b}", tag=f"w_raw{i}_{b}", align_bytes=64)[:]
                 for i, b in ((Y, 0), (Y, 1), (E, 0), (H, 1))}
        pair_raw = keep.tile([P, len(pair), PACK, P], F32, name="pair_raw")
        for n, band in enumerate(pair):
            w_raw[band] = pair_raw[:, n]
        x_rows = xT.rearrange("(p j) t -> p j t", j=PACK)

        def load_w(i, b):
            rows = (w1, w2, w3)[i].rearrange("(p j) n -> p j n", j=PACK)
            nc.sync.dma_start(out=w_raw[i, b], in_=rows[:, :, b * P:(b + 1) * P])

        nc.sync.dma_start(out=planes[0][:], in_=x_rows[:, 0, :])
        nc.sync.dma_start(offs_t[:], offs)
        for j in range(1, LAST):
            nc.sync.dma_start(out=planes[j][:], in_=x_rows[:, j, :])
        for first, last in CHUNKS:
            nc.sync.dma_start(out=planes[LAST][:, first:last], in_=x_rows[:, LAST, first:last])
        for i in (Y, E):
            for b in range(BANDS):
                load_w(i, b)
        nc.sync.dma_start(cen_t[:], cen)
        load_w(H, 0)
        nc.sync.dma_start(pos_t[0][:], pos1)
        load_w(H, 1)
        nc.sync.dma_start(pos_t[1][:], pos2)

        rounded = keep.tile([P, T], BF16, name="rounded")
        grouped = [keep.tile([P, HALF, PACK], BF16, name=f"grouped{u}", align_bytes=64) for u in range(S // HALF)]
        x_scales = keep.tile([P, S], U8, name="x_scales", align_bytes=64)
        w_grouped, w_codes, w_scales = {}, {}, {}
        results = {(i, b): keep.tile([P, S], F32, name=f"result{i}_{b}", align_bytes=64) for i in (Y, E, H) for b in range(BANDS)}
        centre = [keep.tile([P, V], F32, name=f"centre{b}") for b in range(BANDS)]
        total = [keep.tile([P, V], F32, name=f"total{b}") for b in range(BANDS)]
        edges = [(b, d) for b in range(BANDS) for d in range(NEIGHBOURS)]
        message = {(b, d): keep.tile([P, V], F32, name=f"message{b}_{d}") for b, d in edges}
        logit = {(b, d): keep.tile([P, V], F32, name=f"logit{b}_{d}", tag=f"logit{b}_{d}") for b, d in edges[:-1]}
        gate = {(b, d): keep.tile([P, V], F32, name=f"gate{b}_{d}") for b, d in edges}
        fetched = keep.tile([P, V], F32, name="fetched")
        turned = keep.tile([P, V], F32, name="turned")

        def entries(list_tile, first, last):
            return list_tile[:, first // STRIPE:last // STRIPE]

        def gather_x(j, u):
            nc.vector.tensor_copy(grouped[u][:, :, j], planes[j][:].indirect(entries(offs_t, u * HALF, (u + 1) * HALF)))

        def quantize(codes, scales, values):
            nc.vector.quantize_mx(out=codes.bitcast(FP8X4), scales=scales, in_=values.rearrange("p c j -> p (c j)"))

        def quantize_x(first, last):
            u = first // HALF
            quantize(x_codes[:, first:last], x_scales[:, first:last], grouped[u][:, first - u * HALF:last - u * HALF, :])

        def grouped_tile(bands, slot):
            values = keep.tile([P, len(bands) * P, PACK], BF16, name=f"w_grouped{bands[0][0]}_{bands[0][1]}", tag=slot,
                               align_bytes=64)
            for n, band in enumerate(bands):
                w_grouped[band] = values[:, n * P:(n + 1) * P, :]
            return values

        def quantize_w(bands, values, slot):
            name = f"{bands[0][0]}_{bands[0][1]}"
            codes = keep.tile([P, len(bands) * P], U32, name=f"w_codes{name}", tag=slot, align_bytes=64)
            scales = keep.tile([P, len(bands) * P], U8, name=f"w_scales{name}", align_bytes=64)
            for n, band in enumerate(bands):
                w_codes[band] = codes[:, n * P:(n + 1) * P]
                w_scales[band] = scales[:, n * P:(n + 1) * P]
            quantize(codes[:], scales[:], values[:])

        def round_on_gpsimd(dst, src):
            nc.gpsimd.tensor_scalar(dst, src, 1.0, 0.0, MULT, ADD)

        def interleave_on_scalar(i, b):
            nc.scalar.copy(w_grouped[i, b].rearrange("p (c n) j -> p c j n", n=RUN),
                           w_raw[i, b].rearrange("p j (c n) -> p c j n", n=RUN))

        def multiply(i, b, first, last):
            acc = psum.tile([P, BANK], F32, name="acc")
            nc.tensor.matmul_mx(out=acc[:, :last - first], lhsT=w_codes[i, b].bitcast(FP8X4), lhsT_scale=w_scales[i, b],
                                rhs=x_codes[:, first:last].bitcast(FP8X4), rhs_scale=x_scales[:, first:last],
                                start=True, stop=True)
            return acc

        def product(i, b, first, last, copy_out):
            copy_out(results[i, b][:, first:last], multiply(i, b, first, last)[:, :last - first])

        def whole_product(i, b):
            for first in range(0, S, BANK):
                product(i, b, first, first + BANK, nc.scalar.copy)

        def centre_source(b, first, last):
            return results[Y, b][:].indirect(entries(cen_t, first, last))

        def make_logit(b, d):
            nc.vector.tensor_tensor(logit[b, d][:], results[E, b][:].indirect(pos_t[d][:]), centre[b][:], ADD)

        def make_gate(b, d):
            nc.scalar.activation(gate[b, d][:], logit[b, d][:], SIGMOID)

        def make_message(b, d, first, last):
            nc.vector.tensor_tensor(message[b, d][:, first:last], results[H, b][:].indirect(entries(pos_t[d], first, last)),
                                    gate[b, d][:, first:last], MULT)

        def add_turned(b, first, last):
            squares = [slice(c, c + P) for c in range(first, last, P)]
            acc = psum.tile([P, BANK], F32, name="acc")
            for d in range(NEIGHBOURS):
                for c, cols in enumerate(squares):
                    nc.tensor.matmul(acc[:, cols], message[b, d][:, cols], identity[:], is_transpose=True,
                                     start=(d == 0 and c == 0), stop=(d == NEIGHBOURS - 1 and c == len(squares) - 1))
            nc.scalar.copy(turned[:, first:last], acc[:, first:last])

        def turn_back_and_store(b, first, last):
            acc = psum.tile([P, BANK], F32, name="acc")
            for c in range(first, last, P):
                nc.tensor.transpose(acc[:, c:c + P], turned[:, c:c + P], identity[:])
            nc.scalar.copy(total[b][:, first:last], acc[:, first:last])
            nc.sync.dma_start(out=out[b * P:(b + 1) * P, first:last], in_=total[b][:, first:last])

        def add_and_store(b, first, last):
            nc.vector.tensor_tensor(total[b][:, first:last], message[b, 0][:, first:last], message[b, 1][:, first:last], ADD)
            nc.sync.dma_start(out=out[b * P:(b + 1) * P, first:last], in_=total[b][:, first:last])

        for j in range(LAST):
            for u in range(S // HALF):
                gather_x(j, u)
        round_on_gpsimd(rounded[:, slice(*GPSIMD_ROUNDS)], planes[LAST][:, slice(*GPSIMD_ROUNDS)])
        for first, last in SCALAR_ROUNDS:
            nc.scalar.copy(rounded[:, first:last], planes[LAST][:, first:last])
        for first, last in VECTOR_ROUNDS:
            nc.vector.tensor_copy(rounded[:, first:last], planes[LAST][:, first:last])
        gather_x(LAST, 0)
        nc.scalar.activation(grouped[1][:, :, LAST], rounded[:].indirect(entries(offs_t, HALF, S)), COPY)

        y0 = grouped_tile([(Y, 0)], "values_y0")
        y1 = grouped_tile([(Y, 1)], "values_y1")
        e0 = grouped_tile([(E, 0)], "values_e")
        round_on_gpsimd(w_grouped[Y, 0], w_raw[Y, 0].rearrange("p j n -> p n j"))
        quantize_w([(Y, 0)], y0, "codes_y0")
        x_codes = keep.tile([P, S], U32, name="x_codes", tag=f"w_raw{Y}_0", align_bytes=64)
        quantize_x(0, QUARTER)
        quantize_x(QUARTER, HALF)
        quantize_x(HALF, HALF + QUARTER)
        quantize_x(HALF + QUARTER, S - EIGHTH)
        quantize_x(S - EIGHTH, S)
        interleave_on_scalar(Y, 1)
        interleave_on_scalar(E, 0)
        quantize_w([(Y, 1)], y1, "codes_y1")
        product(Y, 0, 0, QUARTER, nc.scalar.copy)
        product(Y, 0, QUARTER, HALF, nc.scalar.copy)
        product(Y, 0, HALF, HALF + QUARTER, nc.vector.tensor_copy)
        product(Y, 0, HALF + QUARTER, S - EIGHTH, nc.scalar.copy)
        product(Y, 0, S - EIGHTH, S, nc.vector.tensor_copy)
        quantize_w([(E, 0)], e0, "codes_y0")
        whole_product(Y, 1)
        whole_product(E, 0)

        pair_values = grouped_tile(pair, "values_e")
        round_on_gpsimd(pair_values[:].rearrange("p (b n) j -> p b n j", b=len(pair)), pair_raw[:].rearrange("p b j n -> p b n j"))
        nc.vector.tensor_copy(centre[0][:], centre_source(0, 0, V))
        nc.vector.tensor_copy(centre[1][:, :SHARE], centre_source(1, 0, SHARE))
        nc.scalar.activation(centre[1][:, SHARE:], centre_source(1, SHARE, V), COPY)
        quantize_w(pair, pair_values, "codes_pair")
        h1 = grouped_tile([(H, 1)], "values_h1")
        interleave_on_scalar(H, 1)
        make_logit(0, 0)
        quantize_w([(H, 1)], h1, "codes_h1")
        make_logit(0, 1)
        for first, last in ((0, QUARTER), (QUARTER, HALF), (HALF, S)):
            product(E, 1, first, last, nc.scalar.copy)
        make_gate(0, 0)
        make_logit(1, 0)
        whole_product(H, 0)
        make_gate(0, 1)

        make_message(0, 0, 0, V)
        for first in (0, MID):
            make_message(0, 1, first, first + MID)
        logit[1, 1] = keep.tile([P, V], F32, name="logit1_1", tag="logit0_1")
        make_logit(1, 1)
        whole_product(H, 1)
        make_gate(1, 0)
        nc.scalar.activation(fetched[:], results[H, 1][:].indirect(pos_t[1][:]), COPY)
        for first in (0, MID):
            add_turned(0, first, first + MID)
        make_gate(1, 1)
        for first in (0, MID):
            turn_back_and_store(0, first, first + MID)
        make_message(1, 0, 0, V)
        for first in (0, MID):
            cols = slice(first, first + MID)
            nc.vector.tensor_tensor(message[1, 1][:, cols], fetched[:, cols], gate[1, 1][:, cols], MULT)
        for first in (0, MID):
            add_and_store(1, first, first + MID)
